import numpy as np
import ml_dtypes


def mxq(x, axis, fmt="e4m3"):
    dtype, down = {"e4m3": (ml_dtypes.float8_e4m3fn, 7), "e5m2": (ml_dtypes.float8_e5m2, 14)}[fmt]
    v = np.moveaxis(np.asarray(x, np.float32).astype(ml_dtypes.bfloat16).astype(np.float64), axis, -1)
    blocks = v.reshape(v.shape[:-1] + (-1, 32))
    amax = np.abs(blocks).max(-1, keepdims=True)
    byte = np.maximum(np.where(amax > 0, np.frexp(amax)[1] - 1 + 127, 0) - down, 1)
    scale = np.exp2(byte - 127.0)
    codes = (blocks / scale).astype(np.float32).astype(dtype).astype(np.float64)
    return np.moveaxis((codes * scale).reshape(v.shape), -1, axis)


WIDE = False


def mx_kscale(k):
    if not WIDE:
        return np.ones(k)
    levels = np.array([10, -10, 5, -5, 0])
    if k % 512:
        return np.exp2(np.random.permutation(np.resize(levels, k // 32))).repeat(32)
    a = np.empty((k // 512, 16))
    for p in range(k // 512):
        a[p, :8] = np.random.permutation(np.resize(levels, 8))
        for g in range(8):
            far = levels[np.abs(levels - a[p, g]) >= 10]
            a[p, g + 8] = far[np.random.randint(len(far))]
    return np.exp2(a.ravel()).repeat(32)


def f64(x):
    return np.asarray(x).astype(np.float64)


def striped(idx):
    return np.tile(idx.reshape(-1, 16).T, (8, 1)).astype(np.uint16)


def unstriped(offs):
    return offs[:16].T.reshape(-1).astype(np.int64)


def pack_weight(w):
    k, n = w.shape
    w = f64(np.asarray(w, np.float32).astype(ml_dtypes.bfloat16)).reshape(k // 32, 32, n)
    amax = np.abs(w).max(1)
    byte = np.clip(np.where(amax > 0, np.frexp(amax)[1] - 1 + 127 - 7, 1), 1, 254)
    scaled = (w * np.exp2(127.0 - byte)[:, None, :]).reshape(k, n).astype(np.float32)
    words = np.ascontiguousarray(scaled.reshape(k // 512, 128, 4, n).transpose(0, 1, 3, 2)).astype(ml_dtypes.float8_e4m3fn).view(np.uint8)
    return words, np.ascontiguousarray(byte.astype(np.uint8).reshape(k // 512, 16, n))


def unpack_weight(words, scales):
    g, p, n, _ = words.shape
    vals = np.ascontiguousarray(words).view(ml_dtypes.float8_e4m3fn).astype(np.float64) * np.repeat(np.exp2(scales.astype(np.float64) - 127.0), 8, axis=1)[..., None]
    return vals.transpose(0, 1, 3, 2).reshape(g * 512, n)


def relu2(v):
    return np.maximum(v, 0.0) ** 2


K, T, S, N = 512, 1024, 512, 256


def setup_inputs():
    n = np.random.standard_normal
    s = mx_kscale(K)[:, None]
    packed = pack_weight(n((K, T)) * s)
    return {
        "x_words": packed[0],
        "x_scales": packed[1],
        "w": (n((K, N)) / np.sqrt(K) / s).astype(np.float32),
        "b": (0.3 * n((N, 1))).astype(np.float32),
        "offs": striped(np.sort(np.random.permutation(T)[:S])),
    }


def reference(x_words, x_scales, w, b, offs):
    idx = unstriped(offs)
    xq = unpack_weight(x_words, x_scales)[:, idx]
    y = mxq(f64(w), 0, "e4m3").T @ xq
    y = relu2(y + f64(b))
    return y

@@ -1,0 +1,98 @@
+from contextlib import ExitStack
+
+import concourse.mybir as mybir
+
+K, T, S, N = 512, 1024, 512, 256
+FLOPS = 2 * K * S * N
+
+F32 = mybir.dt.float32
+BF16 = mybir.dt.bfloat16
+I32 = mybir.dt.int32
+U32 = mybir.dt.uint32
+U16 = mybir.dt.uint16
+U8 = mybir.dt.uint8
+FP8X4 = mybir.dt.float8_e4m3fn_x4
+ACT = mybir.ActivationFunctionType
+ALU = mybir.AluOpType
+
+P = 128
+PACK = 4
+M_TILES = N // P
+CHUNK = 256
+CHUNKS = S // CHUNK
+
+
+def tile_picked_pick_lin_relu2_srt_p_kernel(tc, x_words, x_scales, w, b, offs, out):
+    nc = tc.nc
+    with ExitStack() as ctx:
+        keep = ctx.enter_context(tc.tile_pool(name="keep", bufs=1))
+        psum = ctx.enter_context(tc.psum_pool(name="psum", bufs=1))
+
+        offsets = keep.tile([P, S // 16], U16, name="offsets")
+        w_raw = keep.tile([P, PACK, N], F32, name="w_raw", align_bytes=64)
+        word_table = keep.tile([P, T], I32, name="word_table", align_bytes=64)
+        scale_table = keep.tile([P, T], U8, name="scale_table", align_bytes=64)
+        bias = keep.tile([P, M_TILES, 8], F32, name="bias")
+        warm_in = keep.tile([P, 1], F32, name="warm_in")
+        warm_out = keep.tile([P, 1], F32, name="warm_out")
+
+        nc.vector.memset(scale_table[:].bitcast(I32), 0)
+        nc.vector.memset(warm_in[:], 0.0)
+        nc.scalar.dma_start(out=w_raw[:], in_=w.rearrange("(p t) n -> p t n", t=PACK))
+        nc.sync.dma_start(offsets[:], offs)
+        for q in range(4):
+            nc.sync.dma_start(
+                out=scale_table[32 * q : 32 * q + 4, :].bitcast(I32),
+                in_=x_scales[0, 4 * q : 4 * q + 4, :].bitcast(I32),
+            )
+        nc.sync.dma_start(out=word_table[:], in_=x_words[0].rearrange("p c r -> p (c r)").bitcast(I32))
+        with nc.allow_non_contiguous_dma(reason="one bias value a partition"):
+            nc.scalar.dma_start(out=bias[:, :, 0:1], in_=b.rearrange("(c p) o -> p c o", p=P))
+        nc.scalar.activation(warm_out[:], warm_in[:], ACT.Relu)
+
+        x_scale = keep.tile([P, S], U8, name="x_scale", align_bytes=64)
+        nc.vector.tensor_copy(x_scale[:], scale_table[:].indirect(offsets[:]))
+
+        w_codes, w_scale, grouped = [], [], []
+        for c in range(M_TILES):
+            g = keep.tile([P, P, PACK], BF16, name="grouped%d" % c, align_bytes=64)
+            src = w_raw[:, :, c * P : (c + 1) * P].rearrange("p t m -> p m t")
+            if c == 0:
+                nc.vector.tensor_copy(out=g[:], in_=src)
+            else:
+                nc.scalar.copy(out=g[:], in_=src)
+            grouped.append(g)
+        for c in range(M_TILES):
+            codes = keep.tile([P, P], U32, name="w_codes%d" % c, align_bytes=64)
+            scales = keep.tile([P, P], U8, name="w_scale%d" % c, align_bytes=64)
+            nc.vector.quantize_mx(
+                out=codes[:].bitcast(FP8X4), scales=scales[:], in_=grouped[c][:].rearrange("p m t -> p (m t)")
+            )
+            w_codes.append(codes)
+            w_scale.append(scales)
+
+        x_codes = []
+        for h in range(CHUNKS):
+            xc = keep.tile([P, CHUNK], U32, name="x_codes%d" % h, align_bytes=64)
+            cols = slice(h * CHUNK // 16, (h + 1) * CHUNK // 16)
+            nc.vector.tensor_copy(xc[:], word_table[:].bitcast(U32).indirect(offsets[:, cols]))
+            x_codes.append(xc)
+
+        for h in range(CHUNKS):
+            tok = slice(h * CHUNK, (h + 1) * CHUNK)
+            for c in range(M_TILES):
+                acc = psum.tile([P, CHUNK], F32, name="acc%d_%d" % (h, c))
+                nc.tensor.matmul_mx(
+                    out=acc[:],
+                    lhsT=w_codes[c][:].bitcast(FP8X4),
+                    lhsT_scale=w_scale[c][:],
+                    rhs=x_codes[h][:].bitcast(FP8X4),
+                    rhs_scale=x_scale[:, tok],
+                    start=True,
+                    stop=True,
+                )
+                r = keep.tile([P, CHUNK], F32, name="relu%d_%d" % (h, c))
+                y = keep.tile([P, CHUNK], F32, name="y%d_%d" % (h, c))
+                nc.scalar.activation(r[:], acc[:], ACT.Relu, bias=bias[:, c, 0:1])
+                nc.vector.tensor_tensor(y[:], r[:], r[:], ALU.mult)
+                nc.sync.dma_start(out=out[c * P : (c + 1) * P, tok], in_=y[:])

@@ -18,81 +18,97 @@ ALU = mybir.AluOpType
 P = 128
 PACK = 4
 M_TILES = N // P
-CHUNK = 256
+CHUNK = 128
 CHUNKS = S // CHUNK
+EARLY = T - S + CHUNK
 
 
 def tile_picked_pick_lin_relu2_srt_p_kernel(tc, x_words, x_scales, w, b, offs, out):
     nc = tc.nc
     with ExitStack() as ctx:
         keep = ctx.enter_context(tc.tile_pool(name="keep", bufs=1))
+        shared = ctx.enter_context(tc.tile_pool(name="shared", bufs=1))
         psum = ctx.enter_context(tc.psum_pool(name="psum", bufs=1))
 
         offsets = keep.tile([P, S // 16], U16, name="offsets")
         w_raw = keep.tile([P, PACK, N], F32, name="w_raw", align_bytes=64)
         word_table = keep.tile([P, T], I32, name="word_table", align_bytes=64)
-        scale_table = keep.tile([P, T], U8, name="scale_table", align_bytes=64)
-        bias = keep.tile([P, M_TILES, 8], F32, name="bias")
+        scale_table = shared.tile([P, T], U8, name="scale_table", align_bytes=64, offset=1984)
+        bias = keep.tile([P, M_TILES], F32, name="bias")
         warm_in = keep.tile([P, 1], F32, name="warm_in")
         warm_out = keep.tile([P, 1], F32, name="warm_out")
 
-        nc.vector.memset(scale_table[:].bitcast(I32), 0)
-        nc.vector.memset(warm_in[:], 0.0)
-        nc.scalar.dma_start(out=w_raw[:], in_=w.rearrange("(p t) n -> p t n", t=PACK))
+        words = x_words[0].rearrange("p c r -> p (c r)").bitcast(I32)
         nc.sync.dma_start(offsets[:], offs)
+        nc.scalar.dma_start(out=w_raw[:], in_=w.rearrange("(p t) n -> p t n", t=PACK))
+        nc.vector.memset(scale_table[:].bitcast(I32), 0)
         for q in range(4):
             nc.sync.dma_start(
                 out=scale_table[32 * q : 32 * q + 4, :].bitcast(I32),
                 in_=x_scales[0, 4 * q : 4 * q + 4, :].bitcast(I32),
             )
-        nc.sync.dma_start(out=word_table[:], in_=x_words[0].rearrange("p c r -> p (c r)").bitcast(I32))
-        with nc.allow_non_contiguous_dma(reason="one bias value a partition"):
-            nc.scalar.dma_start(out=bias[:, :, 0:1], in_=b.rearrange("(c p) o -> p c o", p=P))
+        nc.vector.memset(warm_in[:], 0.0)
         nc.scalar.activation(warm_out[:], warm_in[:], ACT.Relu)
+
+        nc.sync.dma_start(out=word_table[:, :EARLY], in_=words[:, :EARLY])
+        nc.sync.dma_start(out=word_table[:, EARLY:], in_=words[:, EARLY:])
+        nc.sync.dma_start(out=bias[:], in_=b.rearrange("(p c) o -> p (c o)", c=M_TILES))
 
         x_scale = keep.tile([P, S], U8, name="x_scale", align_bytes=64)
         nc.vector.tensor_copy(x_scale[:], scale_table[:].indirect(offsets[:]))
 
-        w_codes, w_scale, grouped = [], [], []
-        for c in range(M_TILES):
-            g = keep.tile([P, P, PACK], BF16, name="grouped%d" % c, align_bytes=64)
-            src = w_raw[:, :, c * P : (c + 1) * P].rearrange("p t m -> p m t")
-            if c == 0:
-                nc.vector.tensor_copy(out=g[:], in_=src)
-            else:
-                nc.scalar.copy(out=g[:], in_=src)
-            grouped.append(g)
-        for c in range(M_TILES):
-            codes = keep.tile([P, P], U32, name="w_codes%d" % c, align_bytes=64)
-            scales = keep.tile([P, P], U8, name="w_scale%d" % c, align_bytes=64)
+        x_codes = shared.tile([P, S], U32, name="x_codes", align_bytes=64, offset=0)
+        grouped0 = shared.tile([P, P, PACK], BF16, name="grouped0", align_bytes=64, offset=2944)
+        grouped1 = keep.tile([P, P, PACK], BF16, name="grouped1", align_bytes=64)
+        w_scale0 = keep.tile([P, P], U8, name="w_scale0", align_bytes=64)
+        w_scale1 = shared.tile([P, P], U8, name="w_scale1", align_bytes=64, offset=2048)
+        w_codes0 = keep.tile([P, P], U32, name="w_codes0", align_bytes=64)
+        w_codes1 = keep.tile([P, P], U32, name="w_codes1", align_bytes=64)
+        grouped, w_scale, w_codes = [grouped0, grouped1], [w_scale0, w_scale1], [w_codes0, w_codes1]
+
+        def w_cols(c):
+            return w_raw[:].rearrange("p t (m c) -> p c m t", c=M_TILES)[:, c]
+
+        def quantise(c):
             nc.vector.quantize_mx(
-                out=codes[:].bitcast(FP8X4), scales=scales[:], in_=grouped[c][:].rearrange("p m t -> p (m t)")
+                out=w_codes[c][:].bitcast(FP8X4), scales=w_scale[c][:], in_=grouped[c][:].rearrange("p m t -> p (m t)")
             )
-            w_codes.append(codes)
-            w_scale.append(scales)
 
-        x_codes = []
-        for h in range(CHUNKS):
-            xc = keep.tile([P, CHUNK], U32, name="x_codes%d" % h, align_bytes=64)
-            cols = slice(h * CHUNK // 16, (h + 1) * CHUNK // 16)
-            nc.vector.tensor_copy(xc[:], word_table[:].bitcast(U32).indirect(offsets[:, cols]))
-            x_codes.append(xc)
+        def gather(i):
+            reach = EARLY if i == 0 else T
+            cols = slice(i * CHUNK // 16, (i + 1) * CHUNK // 16)
+            nc.vector.tensor_copy(
+                x_codes[:, i * CHUNK : (i + 1) * CHUNK],
+                word_table[:, :reach].bitcast(U32).indirect(offsets[:, cols]),
+            )
 
-        for h in range(CHUNKS):
-            tok = slice(h * CHUNK, (h + 1) * CHUNK)
+        nc.vector.tensor_copy(out=grouped0[:], in_=w_cols(0))
+        nc.scalar.copy(out=grouped1[:], in_=w_cols(1))
+        gather(0)
+        quantise(0)
+        quantise(1)
+        for i in range(1, CHUNKS):
+            gather(i)
+
+        out_rows = out.rearrange("(p c) s -> p c s", c=M_TILES)
+        for i in range(CHUNKS):
+            tok = slice(i * CHUNK, (i + 1) * CHUNK)
+            y = keep.tile([P, M_TILES, CHUNK], F32, name="y%d" % i)
             for c in range(M_TILES):
-                acc = psum.tile([P, CHUNK], F32, name="acc%d_%d" % (h, c))
+                acc = psum.tile([P, CHUNK], F32, name="acc%d_%d" % (i, c), tag="bank%d_%d" % (i, c))
                 nc.tensor.matmul_mx(
                     out=acc[:],
                     lhsT=w_codes[c][:].bitcast(FP8X4),
                     lhsT_scale=w_scale[c][:],
-                    rhs=x_codes[h][:].bitcast(FP8X4),
+                    rhs=x_codes[:, tok].bitcast(FP8X4),
                     rhs_scale=x_scale[:, tok],
                     start=True,
                     stop=True,
                 )
-                r = keep.tile([P, CHUNK], F32, name="relu%d_%d" % (h, c))
-                y = keep.tile([P, CHUNK], F32, name="y%d_%d" % (h, c))
-                nc.scalar.activation(r[:], acc[:], ACT.Relu, bias=bias[:, c, 0:1])
-                nc.vector.tensor_tensor(y[:], r[:], r[:], ALU.mult)
-                nc.sync.dma_start(out=out[c * P : (c + 1) * P, tok], in_=y[:])
+                r = keep.tile([P, CHUNK], F32, name="relu%d_%d" % (i, c))
+                nc.scalar.activation(r[:], acc[:], ACT.Relu, bias=bias[:, c : c + 1])
+                nc.vector.tensor_tensor(y[:, c, :], r[:], r[:], ALU.mult)
+                if i == CHUNKS - 1:
+                    nc.sync.dma_start(out=out_rows[:, c, tok], in_=y[:, c, :])
+            if i < CHUNKS - 1:
+                nc.sync.dma_start(out=out_rows[:, :, tok], in_=y[:])

@@ -17,98 +17,111 @@ ALU = mybir.AluOpType
 
 P = 128
 PACK = 4
+QUADRANT = 32
+LIST_ROWS = 16
 M_TILES = N // P
 CHUNK = 128
 CHUNKS = S // CHUNK
 EARLY = T - S + CHUNK
+VECTOR_COLUMNS = (64, 96)
+SQUARE_LAG = 2
 
 
 def tile_picked_pick_lin_relu2_srt_p_kernel(tc, x_words, x_scales, w, b, offs, out):
     nc = tc.nc
     with ExitStack() as ctx:
         keep = ctx.enter_context(tc.tile_pool(name="keep", bufs=1))
-        shared = ctx.enter_context(tc.tile_pool(name="shared", bufs=1))
         psum = ctx.enter_context(tc.psum_pool(name="psum", bufs=1))
 
-        offsets = keep.tile([P, S // 16], U16, name="offsets")
+        offsets = keep.tile([P, S // LIST_ROWS], U16, name="offsets")
         w_raw = keep.tile([P, PACK, N], F32, name="w_raw", align_bytes=64)
         word_table = keep.tile([P, T], I32, name="word_table", align_bytes=64)
-        scale_table = shared.tile([P, T], U8, name="scale_table", align_bytes=64, offset=1984)
+        scale_table = keep.tile([P, T], U8, name="scale_table", align_bytes=64)
         bias = keep.tile([P, M_TILES], F32, name="bias")
-        warm_in = keep.tile([P, 1], F32, name="warm_in")
-        warm_out = keep.tile([P, 1], F32, name="warm_out")
+        zero_in = keep.tile([P, 1], F32, name="zero_in")
+        zero = keep.tile([P, 1], F32, name="zero")
 
         words = x_words[0].rearrange("p c r -> p (c r)").bitcast(I32)
         nc.sync.dma_start(offsets[:], offs)
-        nc.scalar.dma_start(out=w_raw[:], in_=w.rearrange("(p t) n -> p t n", t=PACK))
+        nc.scalar.dma_start(out=word_table[:, :EARLY], in_=words[:, :EARLY])
         nc.vector.memset(scale_table[:].bitcast(I32), 0)
-        for q in range(4):
-            nc.sync.dma_start(
-                out=scale_table[32 * q : 32 * q + 4, :].bitcast(I32),
+        for q in range(P // QUADRANT):
+            queue = nc.sync if q < 2 else nc.scalar
+            queue.dma_start(
+                out=scale_table[QUADRANT * q : QUADRANT * q + 4, :].bitcast(I32),
                 in_=x_scales[0, 4 * q : 4 * q + 4, :].bitcast(I32),
             )
-        nc.vector.memset(warm_in[:], 0.0)
-        nc.scalar.activation(warm_out[:], warm_in[:], ACT.Relu)
-
-        nc.sync.dma_start(out=word_table[:, :EARLY], in_=words[:, :EARLY])
+        nc.scalar.dma_start(out=bias[:], in_=b.rearrange("(p c) o -> p (c o)", c=M_TILES))
+        nc.sync.dma_start(out=w_raw[:], in_=w.rearrange("(p t) n -> p t n", t=PACK))
         nc.sync.dma_start(out=word_table[:, EARLY:], in_=words[:, EARLY:])
-        nc.sync.dma_start(out=bias[:], in_=b.rearrange("(p c) o -> p (c o)", c=M_TILES))
+
+        nc.vector.memset(zero_in[:], 0.0)
+        nc.scalar.activation(zero[:], zero_in[:], ACT.Relu)
 
         x_scale = keep.tile([P, S], U8, name="x_scale", align_bytes=64)
+        x_codes = keep.tile([P, S], U32, name="x_codes", align_bytes=64)
+        grouped = [keep.tile([P, P, PACK], BF16, name="grouped%d" % c, align_bytes=64) for c in range(M_TILES)]
+        w_scale = [keep.tile([P, P], U8, name="w_scale%d" % c, align_bytes=64) for c in range(M_TILES)]
+        w_codes = [keep.tile([P, P], U32, name="w_codes%d" % c, align_bytes=64) for c in range(M_TILES)]
+
+        def tokens(i):
+            return slice(i * CHUNK, (i + 1) * CHUNK)
+
+        def gather_words(i):
+            reach = EARLY if i == 0 else T
+            entries = slice(i * CHUNK // LIST_ROWS, (i + 1) * CHUNK // LIST_ROWS)
+            nc.vector.tensor_copy(
+                x_codes[:, tokens(i)], word_table[:, :reach].bitcast(U32).indirect(offsets[:, entries])
+            )
+
+        gather_words(0)
         nc.vector.tensor_copy(x_scale[:], scale_table[:].indirect(offsets[:]))
 
-        x_codes = shared.tile([P, S], U32, name="x_codes", align_bytes=64, offset=0)
-        grouped0 = shared.tile([P, P, PACK], BF16, name="grouped0", align_bytes=64, offset=2944)
-        grouped1 = keep.tile([P, P, PACK], BF16, name="grouped1", align_bytes=64)
-        w_scale0 = keep.tile([P, P], U8, name="w_scale0", align_bytes=64)
-        w_scale1 = shared.tile([P, P], U8, name="w_scale1", align_bytes=64, offset=2048)
-        w_codes0 = keep.tile([P, P], U32, name="w_codes0", align_bytes=64)
-        w_codes1 = keep.tile([P, P], U32, name="w_codes1", align_bytes=64)
-        grouped, w_scale, w_codes = [grouped0, grouped1], [w_scale0, w_scale1], [w_codes0, w_codes1]
-
-        def w_cols(c):
-            return w_raw[:].rearrange("p t (m c) -> p c m t", c=M_TILES)[:, c]
-
-        def quantise(c):
+        w_columns = w_raw[:].rearrange("p t (m c) -> p c m t", c=M_TILES)
+        for c in range(M_TILES):
+            cut = VECTOR_COLUMNS[c]
+            nc.vector.tensor_copy(out=grouped[c][:, :cut, :], in_=w_columns[:, c, :cut, :])
+            nc.scalar.copy(out=grouped[c][:, cut:, :], in_=w_columns[:, c, cut:, :])
+        for c in range(M_TILES):
             nc.vector.quantize_mx(
                 out=w_codes[c][:].bitcast(FP8X4), scales=w_scale[c][:], in_=grouped[c][:].rearrange("p m t -> p (m t)")
             )
-
-        def gather(i):
-            reach = EARLY if i == 0 else T
-            cols = slice(i * CHUNK // 16, (i + 1) * CHUNK // 16)
-            nc.vector.tensor_copy(
-                x_codes[:, i * CHUNK : (i + 1) * CHUNK],
-                word_table[:, :reach].bitcast(U32).indirect(offsets[:, cols]),
-            )
-
-        nc.vector.tensor_copy(out=grouped0[:], in_=w_cols(0))
-        nc.scalar.copy(out=grouped1[:], in_=w_cols(1))
-        gather(0)
-        quantise(0)
-        quantise(1)
         for i in range(1, CHUNKS):
-            gather(i)
+            gather_words(i)
 
         out_rows = out.rearrange("(p c) s -> p c s", c=M_TILES)
-        for i in range(CHUNKS):
-            tok = slice(i * CHUNK, (i + 1) * CHUNK)
-            y = keep.tile([P, M_TILES, CHUNK], F32, name="y%d" % i)
-            for c in range(M_TILES):
-                acc = psum.tile([P, CHUNK], F32, name="acc%d_%d" % (i, c), tag="bank%d_%d" % (i, c))
-                nc.tensor.matmul_mx(
-                    out=acc[:],
-                    lhsT=w_codes[c][:].bitcast(FP8X4),
-                    lhsT_scale=w_scale[c][:],
-                    rhs=x_codes[:, tok].bitcast(FP8X4),
-                    rhs_scale=x_scale[:, tok],
-                    start=True,
-                    stop=True,
-                )
-                r = keep.tile([P, CHUNK], F32, name="relu%d_%d" % (i, c))
-                nc.scalar.activation(r[:], acc[:], ACT.Relu, bias=bias[:, c : c + 1])
-                nc.vector.tensor_tensor(y[:, c, :], r[:], r[:], ALU.mult)
-                if i == CHUNKS - 1:
-                    nc.sync.dma_start(out=out_rows[:, c, tok], in_=y[:, c, :])
-            if i < CHUNKS - 1:
-                nc.sync.dma_start(out=out_rows[:, :, tok], in_=y[:])
+        y = keep.tile([P, M_TILES, S], F32, name="y")
+        relu = keep.tile([P, M_TILES, S], F32, name="relu")
+
+        def multiply(i, c):
+            acc = psum.tile([P, CHUNK], F32, name="acc%d_%d" % (i, c))
+            nc.tensor.matmul_mx(
+                out=acc[:],
+                lhsT=w_codes[c][:].bitcast(FP8X4),
+                lhsT_scale=w_scale[c][:],
+                rhs=x_codes[:, tokens(i)].bitcast(FP8X4),
+                rhs_scale=x_scale[:, tokens(i)],
+                start=True,
+                stop=True,
+            )
+            if i >= CHUNKS // 2 and c == 0:
+                nc.vector.tensor_scalar(relu[:, c, tokens(i)], acc[:], bias[:, c : c + 1], zero[:], ALU.add, ALU.max)
+            else:
+                nc.scalar.activation(relu[:, c, tokens(i)], acc[:], ACT.Relu, bias=bias[:, c : c + 1])
+
+        def square(i, c):
+            r = relu[:, c, tokens(i)]
+            if i == 0 or c == 0:
+                nc.vector.tensor_tensor(y[:, c, tokens(i)], r, r, ALU.mult)
+            else:
+                nc.scalar.activation(y[:, c, tokens(i)], r, ACT.Square)
+            if (i + 1) % (CHUNKS // 2) == 0:
+                half = slice((i + 1) * CHUNK - S // 2, (i + 1) * CHUNK)
+                nc.sync.dma_start(out=out_rows[:, c, half], in_=y[:, c, half])
+
+        passes = [(i, c) for i in range(CHUNKS) for c in range(M_TILES)]
+        for step in range(len(passes) + SQUARE_LAG):
+            if step < len(passes):
+                multiply(*passes[step])
+            if step >= SQUARE_LAG:
+                square(*passes[step - SQUARE_LAG])

@@ -22,9 +22,8 @@ LIST_ROWS = 16
 M_TILES = N // P
 CHUNK = 128
 CHUNKS = S // CHUNK
-EARLY = T - S + CHUNK
-VECTOR_COLUMNS = (64, 96)
-SQUARE_LAG = 2
+EARLY = T - S + 2 * CHUNK
+VECTOR_COLUMNS = 96
 
 
 def tile_picked_pick_lin_relu2_srt_p_kernel(tc, x_words, x_scales, w, b, offs, out):
@@ -51,12 +50,12 @@ def tile_picked_pick_lin_relu2_srt_p_kernel(tc, x_words, x_scales, w, b, offs, o
                 out=scale_table[QUADRANT * q : QUADRANT * q + 4, :].bitcast(I32),
                 in_=x_scales[0, 4 * q : 4 * q + 4, :].bitcast(I32),
             )
-        nc.scalar.dma_start(out=bias[:], in_=b.rearrange("(p c) o -> p (c o)", c=M_TILES))
         nc.sync.dma_start(out=w_raw[:], in_=w.rearrange("(p t) n -> p t n", t=PACK))
+        nc.sync.dma_start(out=bias[:], in_=b.rearrange("(p c) o -> p (c o)", c=M_TILES))
         nc.sync.dma_start(out=word_table[:, EARLY:], in_=words[:, EARLY:])
 
         nc.vector.memset(zero_in[:], 0.0)
-        nc.scalar.activation(zero[:], zero_in[:], ACT.Relu)
+        nc.scalar.activation(zero[:], zero_in[:], ACT.Identity)
 
         x_scale = keep.tile([P, S], U8, name="x_scale", align_bytes=64)
         x_codes = keep.tile([P, S], U32, name="x_codes", align_bytes=64)
@@ -67,33 +66,32 @@ def tile_picked_pick_lin_relu2_srt_p_kernel(tc, x_words, x_scales, w, b, offs, o
         def tokens(i):
             return slice(i * CHUNK, (i + 1) * CHUNK)
 
-        def gather_words(i):
-            reach = EARLY if i == 0 else T
-            entries = slice(i * CHUNK // LIST_ROWS, (i + 1) * CHUNK // LIST_ROWS)
+        def gather_words(first, last, reach):
+            entries = slice(first * CHUNK // LIST_ROWS, last * CHUNK // LIST_ROWS)
             nc.vector.tensor_copy(
-                x_codes[:, tokens(i)], word_table[:, :reach].bitcast(U32).indirect(offsets[:, entries])
+                x_codes[:, first * CHUNK : last * CHUNK],
+                word_table[:, :reach].bitcast(U32).indirect(offsets[:, entries]),
             )
 
-        gather_words(0)
+        gather_words(0, 2, EARLY)
         nc.vector.tensor_copy(x_scale[:], scale_table[:].indirect(offsets[:]))
 
         w_columns = w_raw[:].rearrange("p t (m c) -> p c m t", c=M_TILES)
-        for c in range(M_TILES):
-            cut = VECTOR_COLUMNS[c]
-            nc.vector.tensor_copy(out=grouped[c][:, :cut, :], in_=w_columns[:, c, :cut, :])
-            nc.scalar.copy(out=grouped[c][:, cut:, :], in_=w_columns[:, c, cut:, :])
+        nc.scalar.copy(out=grouped[0][:], in_=w_columns[:, 0])
+        nc.vector.tensor_copy(out=grouped[1][:, :VECTOR_COLUMNS, :], in_=w_columns[:, 1, :VECTOR_COLUMNS, :])
+        nc.scalar.copy(out=grouped[1][:, VECTOR_COLUMNS:, :], in_=w_columns[:, 1, VECTOR_COLUMNS:, :])
         for c in range(M_TILES):
             nc.vector.quantize_mx(
                 out=w_codes[c][:].bitcast(FP8X4), scales=w_scale[c][:], in_=grouped[c][:].rearrange("p m t -> p (m t)")
             )
-        for i in range(1, CHUNKS):
-            gather_words(i)
+        for i in range(2, CHUNKS):
+            gather_words(i, i + 1, T)
 
         out_rows = out.rearrange("(p c) s -> p c s", c=M_TILES)
         y = keep.tile([P, M_TILES, S], F32, name="y")
-        relu = keep.tile([P, M_TILES, S], F32, name="relu")
+        biased = keep.tile([P, M_TILES, S], F32, name="biased")
 
-        def multiply(i, c):
+        def finish(i, c):
             acc = psum.tile([P, CHUNK], F32, name="acc%d_%d" % (i, c))
             nc.tensor.matmul_mx(
                 out=acc[:],
@@ -104,24 +102,22 @@ def tile_picked_pick_lin_relu2_srt_p_kernel(tc, x_words, x_scales, w, b, offs, o
                 start=True,
                 stop=True,
             )
-            if i >= CHUNKS // 2 and c == 0:
-                nc.vector.tensor_scalar(relu[:, c, tokens(i)], acc[:], bias[:, c : c + 1], zero[:], ALU.add, ALU.max)
+            v = biased[:, c, tokens(i)]
+            if (i, c) == (CHUNKS - 1, M_TILES - 1):
+                nc.scalar.activation(v, acc[:], ACT.Relu, bias=bias[:, c : c + 1])
+                nc.scalar.activation(y[:, c, tokens(i)], v, ACT.Square)
             else:
-                nc.scalar.activation(relu[:, c, tokens(i)], acc[:], ACT.Relu, bias=bias[:, c : c + 1])
+                nc.scalar.activation(v, acc[:], ACT.Identity, bias=bias[:, c : c + 1])
+                nc.vector.scalar_tensor_tensor(y[:, c, tokens(i)], v, zero[:], v, ALU.max, ALU.mult)
 
-        def square(i, c):
-            r = relu[:, c, tokens(i)]
-            if i == 0 or c == 0:
-                nc.vector.tensor_tensor(y[:, c, tokens(i)], r, r, ALU.mult)
-            else:
-                nc.scalar.activation(y[:, c, tokens(i)], r, ACT.Square)
-            if (i + 1) % (CHUNKS // 2) == 0:
-                half = slice((i + 1) * CHUNK - S // 2, (i + 1) * CHUNK)
-                nc.sync.dma_start(out=out_rows[:, c, half], in_=y[:, c, half])
-
-        passes = [(i, c) for i in range(CHUNKS) for c in range(M_TILES)]
-        for step in range(len(passes) + SQUARE_LAG):
-            if step < len(passes):
-                multiply(*passes[step])
-            if step >= SQUARE_LAG:
-                square(*passes[step - SQUARE_LAG])
+        for c in range(M_TILES):
+            finish(0, c)
+            finish(1, c)
+            nc.sync.dma_start(out=out_rows[:, c, : 2 * CHUNK], in_=y[:, c, : 2 * CHUNK])
+        for c in range(M_TILES):
+            finish(2, c)
+        nc.sync.dma_start(out=out_rows[:, :, tokens(2)], in_=y[:, :, tokens(2)])
+        finish(3, 0)
+        nc.sync.dma_start(out=out_rows[:, 0, tokens(3)], in_=y[:, 0, tokens(3)])
+        finish(3, 1)
+        nc.scalar.dma_start(out=out_rows[:, 1, tokens(3)], in_=y[:, 1, tokens(3)])

@@ -20,10 +20,11 @@ PACK = 4
 QUADRANT = 32
 LIST_ROWS = 16
 M_TILES = N // P
+LINE = 4
 CHUNK = 128
 CHUNKS = S // CHUNK
 EARLY = T - S + 2 * CHUNK
-VECTOR_COLUMNS = 96
+VECTOR_COLUMNS = (32, 96)
 
 
 def tile_picked_pick_lin_relu2_srt_p_kernel(tc, x_words, x_scales, w, b, offs, out):
@@ -51,43 +52,44 @@ def tile_picked_pick_lin_relu2_srt_p_kernel(tc, x_words, x_scales, w, b, offs, o
                 in_=x_scales[0, 4 * q : 4 * q + 4, :].bitcast(I32),
             )
         nc.sync.dma_start(out=w_raw[:], in_=w.rearrange("(p t) n -> p t n", t=PACK))
-        nc.sync.dma_start(out=bias[:], in_=b.rearrange("(p c) o -> p (c o)", c=M_TILES))
         nc.sync.dma_start(out=word_table[:, EARLY:], in_=words[:, EARLY:])
+        with nc.allow_non_contiguous_dma(reason="two bias values a partition"):
+            nc.sync.dma_start(out=bias[:], in_=b.rearrange("(c p) o -> p (c o)", c=M_TILES))
 
         nc.vector.memset(zero_in[:], 0.0)
         nc.scalar.activation(zero[:], zero_in[:], ACT.Identity)
 
         x_scale = keep.tile([P, S], U8, name="x_scale", align_bytes=64)
-        x_codes = keep.tile([P, S], U32, name="x_codes", align_bytes=64)
-        grouped = [keep.tile([P, P, PACK], BF16, name="grouped%d" % c, align_bytes=64) for c in range(M_TILES)]
+        early_codes = keep.tile([P, S // 2], U32, name="early_codes", align_bytes=64)
+        grouped = [keep.tile([P, P, PACK], BF16, name="grouped%d" % c, tag="stage%d" % c, align_bytes=64) for c in range(M_TILES)]
         w_scale = [keep.tile([P, P], U8, name="w_scale%d" % c, align_bytes=64) for c in range(M_TILES)]
         w_codes = [keep.tile([P, P], U32, name="w_codes%d" % c, align_bytes=64) for c in range(M_TILES)]
 
         def tokens(i):
             return slice(i * CHUNK, (i + 1) * CHUNK)
 
-        def gather_words(first, last, reach):
+        def gather_words(codes, first, last, reach):
             entries = slice(first * CHUNK // LIST_ROWS, last * CHUNK // LIST_ROWS)
-            nc.vector.tensor_copy(
-                x_codes[:, first * CHUNK : last * CHUNK],
-                word_table[:, :reach].bitcast(U32).indirect(offsets[:, entries]),
-            )
+            nc.vector.tensor_copy(codes, word_table[:, :reach].bitcast(U32).indirect(offsets[:, entries]))
 
-        gather_words(0, 2, EARLY)
+        gather_words(early_codes[:], 0, 2, EARLY)
         nc.vector.tensor_copy(x_scale[:], scale_table[:].indirect(offsets[:]))
 
-        w_columns = w_raw[:].rearrange("p t (m c) -> p c m t", c=M_TILES)
-        nc.scalar.copy(out=grouped[0][:], in_=w_columns[:, 0])
-        nc.vector.tensor_copy(out=grouped[1][:, :VECTOR_COLUMNS, :], in_=w_columns[:, 1, :VECTOR_COLUMNS, :])
-        nc.scalar.copy(out=grouped[1][:, VECTOR_COLUMNS:, :], in_=w_columns[:, 1, VECTOR_COLUMNS:, :])
+        w_columns = w_raw[:].rearrange("p t (c j i) -> p c j t i", c=M_TILES, i=LINE)
+        for c in range(M_TILES):
+            cut = VECTOR_COLUMNS[c] // LINE
+            target = grouped[c][:].rearrange("p (j i) t -> p j t i", i=LINE)
+            nc.vector.tensor_copy(out=target[:, :cut], in_=w_columns[:, c, :cut])
+            nc.scalar.copy(out=target[:, cut:], in_=w_columns[:, c, cut:])
         for c in range(M_TILES):
             nc.vector.quantize_mx(
                 out=w_codes[c][:].bitcast(FP8X4), scales=w_scale[c][:], in_=grouped[c][:].rearrange("p m t -> p (m t)")
             )
+        late_codes = keep.tile([P, S // 2], U32, name="late_codes", tag="stage0", align_bytes=64)
         for i in range(2, CHUNKS):
-            gather_words(i, i + 1, T)
+            gather_words(late_codes[:, tokens(i - 2)], i, i + 1, T)
 
-        out_rows = out.rearrange("(p c) s -> p c s", c=M_TILES)
+        out_rows = out.rearrange("(c p) s -> p c s", c=M_TILES)
         y = keep.tile([P, M_TILES, S], F32, name="y")
         biased = keep.tile([P, M_TILES, S], F32, name="biased")
 
@@ -97,7 +99,7 @@ def tile_picked_pick_lin_relu2_srt_p_kernel(tc, x_words, x_scales, w, b, offs, o
                 out=acc[:],
                 lhsT=w_codes[c][:].bitcast(FP8X4),
                 lhsT_scale=w_scale[c][:],
-                rhs=x_codes[:, tokens(i)].bitcast(FP8X4),
+                rhs=(early_codes if i < 2 else late_codes)[:, tokens(i % 2)].bitcast(FP8X4),
                 rhs_scale=x_scale[:, tokens(i)],
                 start=True,
                 stop=True,

@@ -23,8 +23,8 @@ M_TILES = N // P
 LINE = 4
 CHUNK = 128
 CHUNKS = S // CHUNK
-EARLY = T - S + 2 * CHUNK
-VECTOR_COLUMNS = (32, 96)
+EARLY = T - S + CHUNK
+VECTOR_COLUMNS = 80
 
 
 def tile_picked_pick_lin_relu2_srt_p_kernel(tc, x_words, x_scales, w, b, offs, out):
@@ -72,15 +72,16 @@ def tile_picked_pick_lin_relu2_srt_p_kernel(tc, x_words, x_scales, w, b, offs, o
             entries = slice(first * CHUNK // LIST_ROWS, last * CHUNK // LIST_ROWS)
             nc.vector.tensor_copy(codes, word_table[:, :reach].bitcast(U32).indirect(offsets[:, entries]))
 
-        gather_words(early_codes[:], 0, 2, EARLY)
+        gather_words(early_codes[:, tokens(0)], 0, 1, EARLY)
         nc.vector.tensor_copy(x_scale[:], scale_table[:].indirect(offsets[:]))
 
         w_columns = w_raw[:].rearrange("p t (c j i) -> p c j t i", c=M_TILES, i=LINE)
-        for c in range(M_TILES):
-            cut = VECTOR_COLUMNS[c] // LINE
-            target = grouped[c][:].rearrange("p (j i) t -> p j t i", i=LINE)
-            nc.vector.tensor_copy(out=target[:, :cut], in_=w_columns[:, c, :cut])
-            nc.scalar.copy(out=target[:, cut:], in_=w_columns[:, c, cut:])
+        targets = [grouped[c][:].rearrange("p (j i) t -> p j t i", i=LINE) for c in range(M_TILES)]
+        cut = VECTOR_COLUMNS // LINE
+        nc.scalar.copy(out=targets[0], in_=w_columns[:, 0])
+        nc.vector.tensor_copy(out=targets[1][:, :cut], in_=w_columns[:, 1, :cut])
+        nc.scalar.copy(out=targets[1][:, cut:], in_=w_columns[:, 1, cut:])
+        gather_words(early_codes[:, tokens(1)], 1, 2, T)
         for c in range(M_TILES):
             nc.vector.quantize_mx(
                 out=w_codes[c][:].bitcast(FP8X4), scales=w_scale[c][:], in_=grouped[c][:].rearrange("p m t -> p (m t)")

@@ -24,7 +24,7 @@ LINE = 4
 CHUNK = 128
 CHUNKS = S // CHUNK
 EARLY = T - S + CHUNK
-VECTOR_COLUMNS = 80
+SCALAR_COLUMNS = 96
 
 
 def tile_picked_pick_lin_relu2_srt_p_kernel(tc, x_words, x_scales, w, b, offs, out):
@@ -34,7 +34,7 @@ def tile_picked_pick_lin_relu2_srt_p_kernel(tc, x_words, x_scales, w, b, offs, o
         psum = ctx.enter_context(tc.psum_pool(name="psum", bufs=1))
 
         offsets = keep.tile([P, S // LIST_ROWS], U16, name="offsets")
-        w_raw = keep.tile([P, PACK, N], F32, name="w_raw", align_bytes=64)
+        w_raw = keep.tile([P, PACK, N], F32, name="w_raw", tag="raw", align_bytes=64)
         word_table = keep.tile([P, T], I32, name="word_table", align_bytes=64)
         scale_table = keep.tile([P, T], U8, name="scale_table", align_bytes=64)
         bias = keep.tile([P, M_TILES], F32, name="bias")
@@ -43,7 +43,8 @@ def tile_picked_pick_lin_relu2_srt_p_kernel(tc, x_words, x_scales, w, b, offs, o
 
         words = x_words[0].rearrange("p c r -> p (c r)").bitcast(I32)
         nc.sync.dma_start(offsets[:], offs)
-        nc.scalar.dma_start(out=word_table[:, :EARLY], in_=words[:, :EARLY])
+        w_rows = w.rearrange("(p t) n -> p t n", t=PACK)
+        nc.scalar.dma_start(out=w_raw[:, :2], in_=w_rows[:, :2])
         nc.vector.memset(scale_table[:].bitcast(I32), 0)
         for q in range(P // QUADRANT):
             queue = nc.sync if q < 2 else nc.scalar
@@ -51,7 +52,8 @@ def tile_picked_pick_lin_relu2_srt_p_kernel(tc, x_words, x_scales, w, b, offs, o
                 out=scale_table[QUADRANT * q : QUADRANT * q + 4, :].bitcast(I32),
                 in_=x_scales[0, 4 * q : 4 * q + 4, :].bitcast(I32),
             )
-        nc.sync.dma_start(out=w_raw[:], in_=w.rearrange("(p t) n -> p t n", t=PACK))
+        nc.sync.dma_start(out=w_raw[:, 2:], in_=w_rows[:, 2:])
+        nc.sync.dma_start(out=word_table[:, :EARLY], in_=words[:, :EARLY])
         nc.sync.dma_start(out=word_table[:, EARLY:], in_=words[:, EARLY:])
         with nc.allow_non_contiguous_dma(reason="two bias values a partition"):
             nc.sync.dma_start(out=bias[:], in_=b.rearrange("(c p) o -> p (c o)", c=M_TILES))
@@ -60,8 +62,8 @@ def tile_picked_pick_lin_relu2_srt_p_kernel(tc, x_words, x_scales, w, b, offs, o
         nc.scalar.activation(zero[:], zero_in[:], ACT.Identity)
 
         x_scale = keep.tile([P, S], U8, name="x_scale", align_bytes=64)
-        early_codes = keep.tile([P, S // 2], U32, name="early_codes", align_bytes=64)
-        grouped = [keep.tile([P, P, PACK], BF16, name="grouped%d" % c, tag="stage%d" % c, align_bytes=64) for c in range(M_TILES)]
+        early_codes = keep.tile([P, CHUNK], U32, name="early_codes", align_bytes=64)
+        grouped = keep.tile([P, M_TILES, P, PACK], BF16, name="grouped", align_bytes=64)
         w_scale = [keep.tile([P, P], U8, name="w_scale%d" % c, align_bytes=64) for c in range(M_TILES)]
         w_codes = [keep.tile([P, P], U32, name="w_codes%d" % c, align_bytes=64) for c in range(M_TILES)]
 
@@ -72,55 +74,57 @@ def tile_picked_pick_lin_relu2_srt_p_kernel(tc, x_words, x_scales, w, b, offs, o
             entries = slice(first * CHUNK // LIST_ROWS, last * CHUNK // LIST_ROWS)
             nc.vector.tensor_copy(codes, word_table[:, :reach].bitcast(U32).indirect(offsets[:, entries]))
 
-        gather_words(early_codes[:, tokens(0)], 0, 1, EARLY)
         nc.vector.tensor_copy(x_scale[:], scale_table[:].indirect(offsets[:]))
 
         w_columns = w_raw[:].rearrange("p t (c j i) -> p c j t i", c=M_TILES, i=LINE)
-        targets = [grouped[c][:].rearrange("p (j i) t -> p j t i", i=LINE) for c in range(M_TILES)]
-        cut = VECTOR_COLUMNS // LINE
-        nc.scalar.copy(out=targets[0], in_=w_columns[:, 0])
-        nc.vector.tensor_copy(out=targets[1][:, :cut], in_=w_columns[:, 1, :cut])
-        nc.scalar.copy(out=targets[1][:, cut:], in_=w_columns[:, 1, cut:])
-        gather_words(early_codes[:, tokens(1)], 1, 2, T)
+        targets = grouped[:].rearrange("p c (j i) t -> p c j t i", i=LINE)
+        cut = SCALAR_COLUMNS // LINE
+        w_plain = w_raw[:].rearrange("p t (c m) -> p c m t", c=M_TILES)
+        nc.gpsimd.tensor_scalar(grouped[:, :, SCALAR_COLUMNS:], w_plain[:, :, SCALAR_COLUMNS:], 1.0, 0.0, ALU.mult, ALU.add)
+        for c in range(M_TILES):
+            nc.scalar.copy(out=targets[:, c, :cut], in_=w_columns[:, c, :cut])
+        gather_words(early_codes[:, tokens(0)], 0, 1, EARLY)
         for c in range(M_TILES):
             nc.vector.quantize_mx(
-                out=w_codes[c][:].bitcast(FP8X4), scales=w_scale[c][:], in_=grouped[c][:].rearrange("p m t -> p (m t)")
+                out=w_codes[c][:].bitcast(FP8X4), scales=w_scale[c][:], in_=grouped[:, c].rearrange("p m t -> p (m t)")
             )
-        late_codes = keep.tile([P, S // 2], U32, name="late_codes", tag="stage0", align_bytes=64)
-        for i in range(2, CHUNKS):
-            gather_words(late_codes[:, tokens(i - 2)], i, i + 1, T)
+        late_codes = keep.tile([P, S - CHUNK], U32, name="late_codes", tag="raw", align_bytes=64)
+        for i in range(1, CHUNKS):
+            gather_words(late_codes[:, tokens(i - 1)], i, i + 1, T)
 
         out_rows = out.rearrange("(c p) s -> p c s", c=M_TILES)
         y = keep.tile([P, M_TILES, S], F32, name="y")
         biased = keep.tile([P, M_TILES, S], F32, name="biased")
 
-        def finish(i, c):
+        def multiply(i, c):
             acc = psum.tile([P, CHUNK], F32, name="acc%d_%d" % (i, c))
             nc.tensor.matmul_mx(
                 out=acc[:],
                 lhsT=w_codes[c][:].bitcast(FP8X4),
                 lhsT_scale=w_scale[c][:],
-                rhs=(early_codes if i < 2 else late_codes)[:, tokens(i % 2)].bitcast(FP8X4),
+                rhs=(late_codes[:, tokens(i - 1)] if i else early_codes[:]).bitcast(FP8X4),
                 rhs_scale=x_scale[:, tokens(i)],
                 start=True,
                 stop=True,
             )
-            v = biased[:, c, tokens(i)]
-            if (i, c) == (CHUNKS - 1, M_TILES - 1):
-                nc.scalar.activation(v, acc[:], ACT.Relu, bias=bias[:, c : c + 1])
-                nc.scalar.activation(y[:, c, tokens(i)], v, ACT.Square)
-            else:
-                nc.scalar.activation(v, acc[:], ACT.Identity, bias=bias[:, c : c + 1])
-                nc.vector.scalar_tensor_tensor(y[:, c, tokens(i)], v, zero[:], v, ALU.max, ALU.mult)
+            last = (i, c) == (CHUNKS - 1, M_TILES - 1)
+            nc.scalar.activation(biased[:, c, tokens(i)], acc[:], ACT.Relu if last else ACT.Identity, bias=bias[:, c : c + 1])
 
+        def square(i, c):
+            v = biased[:, c, tokens(i)]
+            nc.vector.scalar_tensor_tensor(y[:, c, tokens(i)], v, zero[:], v, ALU.max, ALU.mult)
+
+        for i in range(CHUNKS):
+            for c in range(M_TILES):
+                multiply(i, c)
         for c in range(M_TILES):
-            finish(0, c)
-            finish(1, c)
+            square(0, c)
+            square(1, c)
             nc.sync.dma_start(out=out_rows[:, c, : 2 * CHUNK], in_=y[:, c, : 2 * CHUNK])
         for c in range(M_TILES):
-            finish(2, c)
+            square(2, c)
         nc.sync.dma_start(out=out_rows[:, :, tokens(2)], in_=y[:, :, tokens(2)])
-        finish(3, 0)
+        square(3, 0)
         nc.sync.dma_start(out=out_rows[:, 0, tokens(3)], in_=y[:, 0, tokens(3)])
-        finish(3, 1)
+        nc.scalar.activation(y[:, 1, tokens(3)], biased[:, 1, tokens(3)], ACT.Square)
         nc.scalar.dma_start(out=out_rows[:, 1, tokens(3)], in_=y[:, 1, tokens(3)])

@@ -24,7 +24,7 @@ LINE = 4
 CHUNK = 128
 CHUNKS = S // CHUNK
 EARLY = T - S + CHUNK
-SCALAR_COLUMNS = 96
+SCALAR_COLUMNS = 88
 
 
 def tile_picked_pick_lin_relu2_srt_p_kernel(tc, x_words, x_scales, w, b, offs, out):
@@ -44,7 +44,7 @@ def tile_picked_pick_lin_relu2_srt_p_kernel(tc, x_words, x_scales, w, b, offs, o
         words = x_words[0].rearrange("p c r -> p (c r)").bitcast(I32)
         nc.sync.dma_start(offsets[:], offs)
         w_rows = w.rearrange("(p t) n -> p t n", t=PACK)
-        nc.scalar.dma_start(out=w_raw[:, :2], in_=w_rows[:, :2])
+        nc.sync.dma_start(out=w_raw[:, :2], in_=w_rows[:, :2])
         nc.vector.memset(scale_table[:].bitcast(I32), 0)
         for q in range(P // QUADRANT):
             queue = nc.sync if q < 2 else nc.scalar

@@ -117,13 +117,10 @@ def tile_picked_pick_lin_relu2_srt_p_kernel(tc, x_words, x_scales, w, b, offs, o
         for i in range(CHUNKS):
             for c in range(M_TILES):
                 multiply(i, c)
-        for c in range(M_TILES):
-            square(0, c)
-            square(1, c)
-            nc.sync.dma_start(out=out_rows[:, c, : 2 * CHUNK], in_=y[:, c, : 2 * CHUNK])
-        for c in range(M_TILES):
-            square(2, c)
-        nc.sync.dma_start(out=out_rows[:, :, tokens(2)], in_=y[:, :, tokens(2)])
+        for i in range(CHUNKS - 1):
+            for c in range(M_TILES):
+                square(i, c)
+            nc.sync.dma_start(out=out_rows[:, :, tokens(i)], in_=y[:, :, tokens(i)])
         square(3, 0)
         nc.sync.dma_start(out=out_rows[:, 0, tokens(3)], in_=y[:, 0, tokens(3)])
         nc.scalar.activation(y[:, 1, tokens(3)], biased[:, 1, tokens(3)], ACT.Square)

@@ -107,7 +107,7 @@ def tile_picked_pick_lin_relu2_srt_p_kernel(tc, x_words, x_scales, w, b, offs, o
                 start=True,
                 stop=True,
             )
-            last = (i, c) == (CHUNKS - 1, M_TILES - 1)
+            last = (i, c) == (CHUNKS - 1, 0)
             nc.scalar.activation(biased[:, c, tokens(i)], acc[:], ACT.Relu if last else ACT.Identity, bias=bias[:, c : c + 1])
 
         def square(i, c):
@@ -121,7 +121,7 @@ def tile_picked_pick_lin_relu2_srt_p_kernel(tc, x_words, x_scales, w, b, offs, o
             for c in range(M_TILES):
                 square(i, c)
             nc.sync.dma_start(out=out_rows[:, :, tokens(i)], in_=y[:, :, tokens(i)])
-        square(3, 0)
+        nc.scalar.activation(y[:, 0, tokens(3)], biased[:, 0, tokens(3)], ACT.Square)
         nc.sync.dma_start(out=out_rows[:, 0, tokens(3)], in_=y[:, 0, tokens(3)])
-        nc.scalar.activation(y[:, 1, tokens(3)], biased[:, 1, tokens(3)], ACT.Square)
-        nc.scalar.dma_start(out=out_rows[:, 1, tokens(3)], in_=y[:, 1, tokens(3)])
+        square(3, 1)
+        nc.sync.dma_start(out=out_rows[:, 1, tokens(3)], in_=y[:, 1, tokens(3)])

@@ -24,7 +24,7 @@ LINE = 4
 CHUNK = 128
 CHUNKS = S // CHUNK
 EARLY = T - S + CHUNK
-SCALAR_COLUMNS = 88
+SCALAR_COLUMNS = 200
 
 
 def tile_picked_pick_lin_relu2_srt_p_kernel(tc, x_words, x_scales, w, b, offs, out):
@@ -42,64 +42,82 @@ def tile_picked_pick_lin_relu2_srt_p_kernel(tc, x_words, x_scales, w, b, offs, o
         zero = keep.tile([P, 1], F32, name="zero")
 
         words = x_words[0].rearrange("p c r -> p (c r)").bitcast(I32)
-        nc.sync.dma_start(offsets[:], offs)
         w_rows = w.rearrange("(p t) n -> p t n", t=PACK)
-        nc.sync.dma_start(out=w_raw[:, :2], in_=w_rows[:, :2])
-        nc.vector.memset(scale_table[:].bitcast(I32), 0)
-        for q in range(P // QUADRANT):
-            queue = nc.sync if q < 2 else nc.scalar
+
+        def load_scales(queue, q):
             queue.dma_start(
                 out=scale_table[QUADRANT * q : QUADRANT * q + 4, :].bitcast(I32),
                 in_=x_scales[0, 4 * q : 4 * q + 4, :].bitcast(I32),
             )
+
+        def load_bias(queue):
+            with nc.allow_non_contiguous_dma(reason="two bias values a partition"):
+                queue.dma_start(out=bias[:], in_=b.rearrange("(c p) o -> p (c o)", c=M_TILES))
+
+        nc.sync.dma_start(offsets[:], offs)
+        nc.sync.dma_start(out=w_raw[:, :2], in_=w_rows[:, :2])
+        nc.vector.memset(scale_table[:].bitcast(I32), 0)
+        for q in range(P // QUADRANT):
+            load_scales(nc.sync if q < 2 else nc.scalar, q)
         nc.sync.dma_start(out=w_raw[:, 2:], in_=w_rows[:, 2:])
         nc.sync.dma_start(out=word_table[:, :EARLY], in_=words[:, :EARLY])
         nc.sync.dma_start(out=word_table[:, EARLY:], in_=words[:, EARLY:])
-        with nc.allow_non_contiguous_dma(reason="two bias values a partition"):
-            nc.sync.dma_start(out=bias[:], in_=b.rearrange("(c p) o -> p (c o)", c=M_TILES))
+        load_bias(nc.sync)
 
         nc.vector.memset(zero_in[:], 0.0)
         nc.scalar.activation(zero[:], zero_in[:], ACT.Identity)
 
         x_scale = keep.tile([P, S], U8, name="x_scale", align_bytes=64)
         early_codes = keep.tile([P, CHUNK], U32, name="early_codes", align_bytes=64)
-        grouped = keep.tile([P, M_TILES, P, PACK], BF16, name="grouped", align_bytes=64)
+        grouped = keep.tile([P, M_TILES, P, PACK], BF16, name="grouped", tag="stage", align_bytes=64)
         w_scale = [keep.tile([P, P], U8, name="w_scale%d" % c, align_bytes=64) for c in range(M_TILES)]
         w_codes = [keep.tile([P, P], U32, name="w_codes%d" % c, align_bytes=64) for c in range(M_TILES)]
 
         def tokens(i):
             return slice(i * CHUNK, (i + 1) * CHUNK)
 
-        def gather_words(codes, first, last, reach):
-            entries = slice(first * CHUNK // LIST_ROWS, last * CHUNK // LIST_ROWS)
+        def gather_words(codes, i, reach):
+            entries = slice(i * CHUNK // LIST_ROWS, (i + 1) * CHUNK // LIST_ROWS)
             nc.vector.tensor_copy(codes, word_table[:, :reach].bitcast(U32).indirect(offsets[:, entries]))
 
-        nc.vector.tensor_copy(x_scale[:], scale_table[:].indirect(offsets[:]))
+        w_columns = w_raw[:].rearrange("p t (j i) -> p j t i", i=LINE)
+        targets = grouped[:].rearrange("p c (j i) t -> p (c j) t i", i=LINE)
 
-        w_columns = w_raw[:].rearrange("p t (c j i) -> p c j t i", c=M_TILES, i=LINE)
-        targets = grouped[:].rearrange("p c (j i) t -> p c j t i", i=LINE)
-        cut = SCALAR_COLUMNS // LINE
-        w_plain = w_raw[:].rearrange("p t (c m) -> p c m t", c=M_TILES)
-        nc.gpsimd.tensor_scalar(grouped[:, :, SCALAR_COLUMNS:], w_plain[:, :, SCALAR_COLUMNS:], 1.0, 0.0, ALU.mult, ALU.add)
-        for c in range(M_TILES):
-            nc.scalar.copy(out=targets[:, c, :cut], in_=w_columns[:, c, :cut])
-        gather_words(early_codes[:, tokens(0)], 0, 1, EARLY)
-        for c in range(M_TILES):
+        def interleave(on_scalar, u, first, last):
+            lines, rows = slice(first // LINE, last // LINE), slice(2 * u, 2 * u + 2)
+            if on_scalar:
+                nc.scalar.copy(out=targets[:, lines, rows], in_=w_columns[:, lines, rows])
+            else:
+                nc.gpsimd.tensor_scalar(targets[:, lines, rows], w_columns[:, lines, rows], 1.0, 0.0, ALU.mult, ALU.add)
+
+        def quantize(c):
             nc.vector.quantize_mx(
                 out=w_codes[c][:].bitcast(FP8X4), scales=w_scale[c][:], in_=grouped[:, c].rearrange("p m t -> p (m t)")
             )
+
+        nc.vector.tensor_copy(x_scale[:], scale_table[:].indirect(offsets[:]))
+
+        interleave(True, 0, 0, SCALAR_COLUMNS)
+        interleave(False, 0, SCALAR_COLUMNS, N)
+        interleave(True, 1, 0, P)
+        interleave(False, 1, SCALAR_COLUMNS, N)
+        interleave(True, 1, P, SCALAR_COLUMNS)
+        quantize(0)
+        gather_words(early_codes[:], 0, EARLY)
+        quantize(1)
         late_codes = keep.tile([P, S - CHUNK], U32, name="late_codes", tag="raw", align_bytes=64)
         for i in range(1, CHUNKS):
-            gather_words(late_codes[:, tokens(i - 1)], i, i + 1, T)
+            gather_words(late_codes[:, tokens(i - 1)], i, T)
 
         out_rows = out.rearrange("(c p) s -> p c s", c=M_TILES)
-        y = keep.tile([P, M_TILES, S], F32, name="y")
+        y = keep.tile([P, M_TILES, S], F32, name="y", tag="stage", align_bytes=64)
         biased = keep.tile([P, M_TILES, S], F32, name="biased")
+        acc = {}
 
         def multiply(i, c):
-            acc = psum.tile([P, CHUNK], F32, name="acc%d_%d" % (i, c))
+            acc[i, c] = psum.tile([P, CHUNK], F32, name="acc%d_%d" % (i, c))
             nc.tensor.matmul_mx(
-                out=acc[:],
+                out=acc[i, c][:],
                 lhsT=w_codes[c][:].bitcast(FP8X4),
                 lhsT_scale=w_scale[c][:],
                 rhs=(late_codes[:, tokens(i - 1)] if i else early_codes[:]).bitcast(FP8X4),
@@ -107,21 +125,24 @@ def tile_picked_pick_lin_relu2_srt_p_kernel(tc, x_words, x_scales, w, b, offs, o
                 start=True,
                 stop=True,
             )
-            last = (i, c) == (CHUNKS - 1, 0)
-            nc.scalar.activation(biased[:, c, tokens(i)], acc[:], ACT.Relu if last else ACT.Identity, bias=bias[:, c : c + 1])
+
+        def add_bias(i, c, func):
+            nc.scalar.activation(biased[:, c, tokens(i)], acc[i, c][:], func, bias=bias[:, c : c + 1])
 
         def square(i, c):
             v = biased[:, c, tokens(i)]
             nc.vector.scalar_tensor_tensor(y[:, c, tokens(i)], v, zero[:], v, ALU.max, ALU.mult)
 
+        last = CHUNKS - 1
         for i in range(CHUNKS):
             for c in range(M_TILES):
                 multiply(i, c)
-        for i in range(CHUNKS - 1):
+                add_bias(i, c, ACT.Relu if (i, c) == (last, 0) else ACT.Identity)
+        for i in range(last):
             for c in range(M_TILES):
                 square(i, c)
             nc.sync.dma_start(out=out_rows[:, :, tokens(i)], in_=y[:, :, tokens(i)])
-        nc.scalar.activation(y[:, 0, tokens(3)], biased[:, 0, tokens(3)], ACT.Square)
-        nc.sync.dma_start(out=out_rows[:, 0, tokens(3)], in_=y[:, 0, tokens(3)])
-        square(3, 1)
-        nc.sync.dma_start(out=out_rows[:, 1, tokens(3)], in_=y[:, 1, tokens(3)])
+        nc.scalar.activation(y[:, 0, tokens(last)], biased[:, 0, tokens(last)], ACT.Square)
+        nc.sync.dma_start(out=out_rows[:, 0, tokens(last)], in_=y[:, 0, tokens(last)])
+        square(last, 1)
+        nc.sync.dma_start(out=out_rows[:, 1, tokens(last)], in_=y[:, 1, tokens(last)])

@@ -58,7 +58,7 @@ def tile_picked_pick_lin_relu2_srt_p_kernel(tc, x_words, x_scales, w, b, offs, o
         nc.sync.dma_start(out=w_raw[:, :2], in_=w_rows[:, :2])
         nc.vector.memset(scale_table[:].bitcast(I32), 0)
         for q in range(P // QUADRANT):
-            load_scales(nc.sync if q < 2 else nc.scalar, q)
+            load_scales(nc.sync if q else nc.scalar, q)
         nc.sync.dma_start(out=w_raw[:, 2:], in_=w_rows[:, 2:])
         nc.sync.dma_start(out=word_table[:, :EARLY], in_=words[:, :EARLY])
         nc.sync.dma_start(out=word_table[:, EARLY:], in_=words[:, EARLY:])

@@ -54,11 +54,13 @@ def tile_picked_pick_lin_relu2_srt_p_kernel(tc, x_words, x_scales, w, b, offs, o
             with nc.allow_non_contiguous_dma(reason="two bias values a partition"):
                 queue.dma_start(out=bias[:], in_=b.rearrange("(c p) o -> p (c o)", c=M_TILES))
 
-        nc.sync.dma_start(offsets[:], offs)
+        first_rows = keep.tile([4, T // PACK], I32, name="first_rows", align_bytes=64)
+        nc.scalar.dma_start(out=first_rows[:], in_=x_scales[0, 0:4, :].bitcast(I32))
         nc.sync.dma_start(out=w_raw[:, :2], in_=w_rows[:, :2])
+        nc.sync.dma_start(offsets[:], offs)
         nc.vector.memset(scale_table[:].bitcast(I32), 0)
-        for q in range(P // QUADRANT):
-            load_scales(nc.sync if q else nc.scalar, q)
+        for q in range(1, P // QUADRANT):
+            load_scales(nc.sync, q)
         nc.sync.dma_start(out=w_raw[:, 2:], in_=w_rows[:, 2:])
         nc.sync.dma_start(out=word_table[:, :EARLY], in_=words[:, :EARLY])
         nc.sync.dma_start(out=word_table[:, EARLY:], in_=words[:, EARLY:])
@@ -95,6 +97,7 @@ def tile_picked_pick_lin_relu2_srt_p_kernel(tc, x_words, x_scales, w, b, offs, o
                 out=w_codes[c][:].bitcast(FP8X4), scales=w_scale[c][:], in_=grouped[:, c].rearrange("p m t -> p (m t)")
             )
 
+        nc.vector.tensor_copy(scale_table[0:4, :].bitcast(I32), first_rows[:])
         nc.vector.tensor_copy(x_scale[:], scale_table[:].indirect(offsets[:]))
 
         interleave(True, 0, 0, SCALAR_COLUMNS)

@@ -21,6 +21,7 @@ QUADRANT = 32
 LIST_ROWS = 16
 M_TILES = N // P
 LINE = 4
+BLOCK = 8
 CHUNK = 128
 CHUNKS = S // CHUNK
 EARLY = T - S + CHUNK
@@ -37,7 +38,7 @@ def tile_picked_pick_lin_relu2_srt_p_kernel(tc, x_words, x_scales, w, b, offs, o
         w_raw = keep.tile([P, PACK, N], F32, name="w_raw", tag="raw", align_bytes=64)
         word_table = keep.tile([P, T], I32, name="word_table", align_bytes=64)
         scale_table = keep.tile([P, T], U8, name="scale_table", align_bytes=64)
-        bias = keep.tile([P, M_TILES], F32, name="bias")
+        bias = keep.tile([P, M_TILES, BLOCK], F32, name="bias")
         zero_in = keep.tile([P, 1], F32, name="zero_in")
         zero = keep.tile([P, 1], F32, name="zero")
 
@@ -52,7 +53,7 @@ def tile_picked_pick_lin_relu2_srt_p_kernel(tc, x_words, x_scales, w, b, offs, o
 
         def load_bias(queue):
             with nc.allow_non_contiguous_dma(reason="two bias values a partition"):
-                queue.dma_start(out=bias[:], in_=b.rearrange("(c p) o -> p (c o)", c=M_TILES))
+                queue.dma_start(out=bias[:, :, 0:1], in_=b.rearrange("(c p) o -> p c o", c=M_TILES))
 
         first_rows = keep.tile([4, T // PACK], I32, name="first_rows", align_bytes=64)
         nc.scalar.dma_start(out=first_rows[:], in_=x_scales[0, 0:4, :].bitcast(I32))
@@ -130,21 +131,25 @@ def tile_picked_pick_lin_relu2_srt_p_kernel(tc, x_words, x_scales, w, b, offs, o
             )
 
         def add_bias(i, c, func):
-            nc.scalar.activation(biased[:, c, tokens(i)], acc[i, c][:], func, bias=bias[:, c : c + 1])
+            nc.scalar.activation(biased[:, c, tokens(i)], acc[i, c][:], func, bias=bias[:, c, 0:1])
 
         def square(i, c):
             v = biased[:, c, tokens(i)]
             nc.vector.scalar_tensor_tensor(y[:, c, tokens(i)], v, zero[:], v, ALU.max, ALU.mult)
 
         last = CHUNKS - 1
-        for i in range(CHUNKS):
-            for c in range(M_TILES):
-                multiply(i, c)
-                add_bias(i, c, ACT.Relu if (i, c) == (last, 0) else ACT.Identity)
-        for i in range(last):
-            for c in range(M_TILES):
+        middle = range(1, last)
+        order = [(0, c) for c in range(M_TILES)] + [(i, c) for c in range(M_TILES) for i in middle] + [(last, c) for c in range(M_TILES)]
+        for i, c in order:
+            multiply(i, c)
+            add_bias(i, c, ACT.Relu if (i, c) == (last, 0) else ACT.Identity)
+        for c in range(M_TILES):
+            square(0, c)
+        nc.sync.dma_start(out=out_rows[:, :, tokens(0)], in_=y[:, :, tokens(0)])
+        for c in range(M_TILES):
+            for i in middle:
                 square(i, c)
-            nc.sync.dma_start(out=out_rows[:, :, tokens(i)], in_=y[:, :, tokens(i)])
+            nc.sync.dma_start(out=out_rows[:, c, CHUNK : S - CHUNK], in_=y[:, c, CHUNK : S - CHUNK])
         nc.scalar.activation(y[:, 0, tokens(last)], biased[:, 0, tokens(last)], ACT.Square)
         nc.sync.dma_start(out=out_rows[:, 0, tokens(last)], in_=y[:, 0, tokens(last)])
         square(last, 1)

@@ -21,11 +21,12 @@ QUADRANT = 32
 LIST_ROWS = 16
 M_TILES = N // P
 LINE = 4
+STAGED = 2
 BLOCK = 8
 CHUNK = 128
 CHUNKS = S // CHUNK
 EARLY = T - S + CHUNK
-SCALAR_COLUMNS = 200
+SCALAR_COLUMNS = 216
 
 
 def tile_picked_pick_lin_relu2_srt_p_kernel(tc, x_words, x_scales, w, b, offs, out):
@@ -55,12 +56,13 @@ def tile_picked_pick_lin_relu2_srt_p_kernel(tc, x_words, x_scales, w, b, offs, o
             with nc.allow_non_contiguous_dma(reason="two bias values a partition"):
                 queue.dma_start(out=bias[:, :, 0:1], in_=b.rearrange("(c p) o -> p c o", c=M_TILES))
 
-        first_rows = keep.tile([4, T // PACK], I32, name="first_rows", align_bytes=64)
-        nc.scalar.dma_start(out=first_rows[:], in_=x_scales[0, 0:4, :].bitcast(I32))
+        staged = slice(QUADRANT * STAGED, QUADRANT * STAGED + 4)
+        first_rows = keep.tile([P, T // PACK], I32, name="first_rows", align_bytes=64)
+        nc.scalar.dma_start(out=first_rows[staged, :], in_=x_scales[0, 4 * STAGED : 4 * STAGED + 4, :].bitcast(I32))
         nc.sync.dma_start(out=w_raw[:, :2], in_=w_rows[:, :2])
         nc.sync.dma_start(offsets[:], offs)
         nc.vector.memset(scale_table[:].bitcast(I32), 0)
-        for q in range(1, P // QUADRANT):
+        for q in (0, 3, 1):
             load_scales(nc.sync, q)
         nc.sync.dma_start(out=w_raw[:, 2:], in_=w_rows[:, 2:])
         nc.sync.dma_start(out=word_table[:, :EARLY], in_=words[:, :EARLY])
@@ -98,7 +100,7 @@ def tile_picked_pick_lin_relu2_srt_p_kernel(tc, x_words, x_scales, w, b, offs, o
                 out=w_codes[c][:].bitcast(FP8X4), scales=w_scale[c][:], in_=grouped[:, c].rearrange("p m t -> p (m t)")
             )
 
-        nc.vector.tensor_copy(scale_table[0:4, :].bitcast(I32), first_rows[:])
+        nc.vector.tensor_copy(scale_table[staged, :].bitcast(I32), first_rows[staged, :])
         nc.vector.tensor_copy(x_scale[:], scale_table[:].indirect(offsets[:]))
 
         interleave(True, 0, 0, SCALAR_COLUMNS)
@@ -145,7 +147,7 @@ def tile_picked_pick_lin_relu2_srt_p_kernel(tc, x_words, x_scales, w, b, offs, o
             add_bias(i, c, ACT.Relu if (i, c) == (last, 0) else ACT.Identity)
         for c in range(M_TILES):
             square(0, c)
-        nc.sync.dma_start(out=out_rows[:, :, tokens(0)], in_=y[:, :, tokens(0)])
+            nc.sync.dma_start(out=out_rows[:, c, tokens(0)], in_=y[:, c, tokens(0)])
         for c in range(M_TILES):
             for i in middle:
                 square(i, c)

@@ -25,8 +25,15 @@ STAGED = 2
 BLOCK = 8
 CHUNK = 128
 CHUNKS = S // CHUNK
-EARLY = T - S + CHUNK
 SCALAR_COLUMNS = 216
+
+
+def reach(i):
+    return T - S + (i + 1) * CHUNK
+
+
+def tokens(first, last=None):
+    return slice(first * CHUNK, ((first if last is None else last) + 1) * CHUNK)
 
 
 def tile_picked_pick_lin_relu2_srt_p_kernel(tc, x_words, x_scales, w, b, offs, out):
@@ -39,6 +46,7 @@ def tile_picked_pick_lin_relu2_srt_p_kernel(tc, x_words, x_scales, w, b, offs, o
         w_raw = keep.tile([P, PACK, N], F32, name="w_raw", tag="raw", align_bytes=64)
         word_table = keep.tile([P, T], I32, name="word_table", align_bytes=64)
         scale_table = keep.tile([P, T], U8, name="scale_table", align_bytes=64)
+        first_rows = keep.tile([P, T // PACK], I32, name="first_rows", align_bytes=64)
         bias = keep.tile([P, M_TILES, BLOCK], F32, name="bias")
         zero_in = keep.tile([P, 1], F32, name="zero_in")
         zero = keep.tile([P, 1], F32, name="zero")
@@ -46,28 +54,23 @@ def tile_picked_pick_lin_relu2_srt_p_kernel(tc, x_words, x_scales, w, b, offs, o
         words = x_words[0].rearrange("p c r -> p (c r)").bitcast(I32)
         w_rows = w.rearrange("(p t) n -> p t n", t=PACK)
 
-        def load_scales(queue, q):
-            queue.dma_start(
-                out=scale_table[QUADRANT * q : QUADRANT * q + 4, :].bitcast(I32),
-                in_=x_scales[0, 4 * q : 4 * q + 4, :].bitcast(I32),
-            )
+        def live(q):
+            return slice(QUADRANT * q, QUADRANT * q + 4)
 
-        def load_bias(queue):
-            with nc.allow_non_contiguous_dma(reason="two bias values a partition"):
-                queue.dma_start(out=bias[:, :, 0:1], in_=b.rearrange("(c p) o -> p c o", c=M_TILES))
+        def scale_rows(q):
+            return x_scales[0, 4 * q : 4 * q + 4, :].bitcast(I32)
 
-        staged = slice(QUADRANT * STAGED, QUADRANT * STAGED + 4)
-        first_rows = keep.tile([P, T // PACK], I32, name="first_rows", align_bytes=64)
-        nc.scalar.dma_start(out=first_rows[staged, :], in_=x_scales[0, 4 * STAGED : 4 * STAGED + 4, :].bitcast(I32))
+        nc.scalar.dma_start(out=first_rows[live(STAGED), :], in_=scale_rows(STAGED))
         nc.sync.dma_start(out=w_raw[:, :2], in_=w_rows[:, :2])
         nc.sync.dma_start(offsets[:], offs)
         nc.vector.memset(scale_table[:].bitcast(I32), 0)
         for q in (0, 3, 1):
-            load_scales(nc.sync, q)
+            nc.sync.dma_start(out=scale_table[live(q), :].bitcast(I32), in_=scale_rows(q))
         nc.sync.dma_start(out=w_raw[:, 2:], in_=w_rows[:, 2:])
-        nc.sync.dma_start(out=word_table[:, :EARLY], in_=words[:, :EARLY])
-        nc.sync.dma_start(out=word_table[:, EARLY:], in_=words[:, EARLY:])
-        load_bias(nc.sync)
+        for first, last in ((0, reach(0)), (reach(0), reach(2)), (reach(2), T)):
+            nc.sync.dma_start(out=word_table[:, first:last], in_=words[:, first:last])
+        with nc.allow_non_contiguous_dma(reason="two bias values a partition"):
+            nc.sync.dma_start(out=bias[:, :, 0:1], in_=b.rearrange("(c p) o -> p c o", c=M_TILES))
 
         nc.vector.memset(zero_in[:], 0.0)
         nc.scalar.activation(zero[:], zero_in[:], ACT.Identity)
@@ -78,12 +81,9 @@ def tile_picked_pick_lin_relu2_srt_p_kernel(tc, x_words, x_scales, w, b, offs, o
         w_scale = [keep.tile([P, P], U8, name="w_scale%d" % c, align_bytes=64) for c in range(M_TILES)]
         w_codes = [keep.tile([P, P], U32, name="w_codes%d" % c, align_bytes=64) for c in range(M_TILES)]
 
-        def tokens(i):
-            return slice(i * CHUNK, (i + 1) * CHUNK)
-
-        def gather_words(codes, i, reach):
+        def gather_words(codes, i):
             entries = slice(i * CHUNK // LIST_ROWS, (i + 1) * CHUNK // LIST_ROWS)
-            nc.vector.tensor_copy(codes, word_table[:, :reach].bitcast(U32).indirect(offsets[:, entries]))
+            nc.vector.tensor_copy(codes, word_table[:, : reach(i)].bitcast(U32).indirect(offsets[:, entries]))
 
         w_columns = w_raw[:].rearrange("p t (j i) -> p j t i", i=LINE)
         targets = grouped[:].rearrange("p c (j i) t -> p (c j) t i", i=LINE)
@@ -100,7 +100,7 @@ def tile_picked_pick_lin_relu2_srt_p_kernel(tc, x_words, x_scales, w, b, offs, o
                 out=w_codes[c][:].bitcast(FP8X4), scales=w_scale[c][:], in_=grouped[:, c].rearrange("p m t -> p (m t)")
             )
 
-        nc.vector.tensor_copy(scale_table[staged, :].bitcast(I32), first_rows[staged, :])
+        nc.vector.tensor_copy(scale_table[live(STAGED), :].bitcast(I32), first_rows[live(STAGED), :])
         nc.vector.tensor_copy(x_scale[:], scale_table[:].indirect(offsets[:]))
 
         interleave(True, 0, 0, SCALAR_COLUMNS)
@@ -109,21 +109,21 @@ def tile_picked_pick_lin_relu2_srt_p_kernel(tc, x_words, x_scales, w, b, offs, o
         interleave(False, 1, SCALAR_COLUMNS, N)
         interleave(True, 1, P, SCALAR_COLUMNS)
         quantize(0)
-        gather_words(early_codes[:], 0, EARLY)
+        gather_words(early_codes[:], 0)
         quantize(1)
         late_codes = keep.tile([P, S - CHUNK], U32, name="late_codes", tag="raw", align_bytes=64)
         for i in range(1, CHUNKS):
-            gather_words(late_codes[:, tokens(i - 1)], i, T)
+            gather_words(late_codes[:, tokens(i - 1)], i)
 
         out_rows = out.rearrange("(c p) s -> p c s", c=M_TILES)
         y = keep.tile([P, M_TILES, S], F32, name="y", tag="stage", align_bytes=64)
         biased = keep.tile([P, M_TILES, S], F32, name="biased")
-        acc = {}
 
-        def multiply(i, c):
-            acc[i, c] = psum.tile([P, CHUNK], F32, name="acc%d_%d" % (i, c))
+        order = [(i, c if i % 2 == 0 else M_TILES - 1 - c) for i in range(CHUNKS) for c in range(M_TILES)]
+        for i, c in order:
+            acc = psum.tile([P, CHUNK], F32, name="acc%d_%d" % (i, c))
             nc.tensor.matmul_mx(
-                out=acc[i, c][:],
+                out=acc[:],
                 lhsT=w_codes[c][:].bitcast(FP8X4),
                 lhsT_scale=w_scale[c][:],
                 rhs=(late_codes[:, tokens(i - 1)] if i else early_codes[:]).bitcast(FP8X4),
@@ -131,28 +131,13 @@ def tile_picked_pick_lin_relu2_srt_p_kernel(tc, x_words, x_scales, w, b, offs, o
                 start=True,
                 stop=True,
             )
+            nc.scalar.activation(biased[:, c, tokens(i)], acc[:], ACT.Identity, bias=bias[:, c, 0:1])
 
-        def add_bias(i, c, func):
-            nc.scalar.activation(biased[:, c, tokens(i)], acc[i, c][:], func, bias=bias[:, c, 0:1])
-
-        def square(i, c):
+        stored = [0] * M_TILES
+        for n, (i, c) in enumerate(order):
             v = biased[:, c, tokens(i)]
             nc.vector.scalar_tensor_tensor(y[:, c, tokens(i)], v, zero[:], v, ALU.max, ALU.mult)
-
-        last = CHUNKS - 1
-        middle = range(1, last)
-        order = [(0, c) for c in range(M_TILES)] + [(i, c) for c in range(M_TILES) for i in middle] + [(last, c) for c in range(M_TILES)]
-        for i, c in order:
-            multiply(i, c)
-            add_bias(i, c, ACT.Relu if (i, c) == (last, 0) else ACT.Identity)
-        for c in range(M_TILES):
-            square(0, c)
-            nc.sync.dma_start(out=out_rows[:, c, tokens(0)], in_=y[:, c, tokens(0)])
-        for c in range(M_TILES):
-            for i in middle:
-                square(i, c)
-            nc.sync.dma_start(out=out_rows[:, c, CHUNK : S - CHUNK], in_=y[:, c, CHUNK : S - CHUNK])
-        nc.scalar.activation(y[:, 0, tokens(last)], biased[:, 0, tokens(last)], ACT.Square)
-        nc.sync.dma_start(out=out_rows[:, 0, tokens(last)], in_=y[:, 0, tokens(last)])
-        square(last, 1)
-        nc.sync.dma_start(out=out_rows[:, 1, tokens(last)], in_=y[:, 1, tokens(last)])
+            if n + 1 == len(order) or order[n + 1][1] != c:
+                run = tokens(stored[c], i)
+                nc.sync.dma_start(out=out_rows[:, c, run], in_=y[:, c, run])
+                stored[c] = i + 1

@@ -67,10 +67,11 @@ def tile_picked_pick_lin_relu2_srt_p_kernel(tc, x_words, x_scales, w, b, offs, o
         for q in (0, 3, 1):
             nc.sync.dma_start(out=scale_table[live(q), :].bitcast(I32), in_=scale_rows(q))
         nc.sync.dma_start(out=w_raw[:, 2:], in_=w_rows[:, 2:])
-        for first, last in ((0, reach(0)), (reach(0), reach(2)), (reach(2), T)):
+        for first, last in ((0, reach(0)), (reach(0), reach(2))):
             nc.sync.dma_start(out=word_table[:, first:last], in_=words[:, first:last])
         with nc.allow_non_contiguous_dma(reason="two bias values a partition"):
             nc.sync.dma_start(out=bias[:, :, 0:1], in_=b.rearrange("(c p) o -> p c o", c=M_TILES))
+        nc.sync.dma_start(out=word_table[:, reach(2) :], in_=words[:, reach(2) :])
 
         nc.vector.memset(zero_in[:], 0.0)
         nc.scalar.activation(zero[:], zero_in[:], ACT.Identity)

@@ -132,12 +132,15 @@ def tile_picked_pick_lin_relu2_srt_p_kernel(tc, x_words, x_scales, w, b, offs, o
                 start=True,
                 stop=True,
             )
-            nc.scalar.activation(biased[:, c, tokens(i)], acc[:], ACT.Identity, bias=bias[:, c, 0:1])
+            nc.scalar.activation(biased[:, c, tokens(i)], acc[:], ACT.Relu, bias=bias[:, c, 0:1])
 
         stored = [0] * M_TILES
         for n, (i, c) in enumerate(order):
             v = biased[:, c, tokens(i)]
-            nc.vector.scalar_tensor_tensor(y[:, c, tokens(i)], v, zero[:], v, ALU.max, ALU.mult)
+            if n == len(order) - 2:
+                nc.scalar.activation(y[:, c, tokens(i)], v, ACT.Square, bias=zero[:])
+            else:
+                nc.vector.tensor_tensor(y[:, c, tokens(i)], v, v, ALU.mult)
             if n + 1 == len(order) or order[n + 1][1] != c:
                 run = tokens(stored[c], i)
                 nc.sync.dma_start(out=out_rows[:, c, run], in_=y[:, c, run])

@@ -25,7 +25,7 @@ STAGED = 2
 BLOCK = 8
 CHUNK = 128
 CHUNKS = S // CHUNK
-SCALAR_COLUMNS = 216
+SCALAR_COLUMNS = 80
 
 
 def reach(i):
@@ -67,11 +67,10 @@ def tile_picked_pick_lin_relu2_srt_p_kernel(tc, x_words, x_scales, w, b, offs, o
         for q in (0, 3, 1):
             nc.sync.dma_start(out=scale_table[live(q), :].bitcast(I32), in_=scale_rows(q))
         nc.sync.dma_start(out=w_raw[:, 2:], in_=w_rows[:, 2:])
-        for first, last in ((0, reach(0)), (reach(0), reach(2))):
+        for first, last in ((0, reach(0)), (reach(0), reach(2)), (reach(2), T)):
             nc.sync.dma_start(out=word_table[:, first:last], in_=words[:, first:last])
         with nc.allow_non_contiguous_dma(reason="two bias values a partition"):
             nc.sync.dma_start(out=bias[:, :, 0:1], in_=b.rearrange("(c p) o -> p c o", c=M_TILES))
-        nc.sync.dma_start(out=word_table[:, reach(2) :], in_=words[:, reach(2) :])
 
         nc.vector.memset(zero_in[:], 0.0)
         nc.scalar.activation(zero[:], zero_in[:], ACT.Identity)
@@ -86,15 +85,14 @@ def tile_picked_pick_lin_relu2_srt_p_kernel(tc, x_words, x_scales, w, b, offs, o
             entries = slice(i * CHUNK // LIST_ROWS, (i + 1) * CHUNK // LIST_ROWS)
             nc.vector.tensor_copy(codes, word_table[:, : reach(i)].bitcast(U32).indirect(offsets[:, entries]))
 
-        w_columns = w_raw[:].rearrange("p t (j i) -> p j t i", i=LINE)
-        targets = grouped[:].rearrange("p c (j i) t -> p (c j) t i", i=LINE)
+        w_columns = w_raw[:].rearrange("p t (c j i) -> p c j t i", c=M_TILES, i=LINE)
+        targets = grouped[:].rearrange("p c (j i) t -> p c j t i", i=LINE)
+        split = SCALAR_COLUMNS // LINE
 
-        def interleave(on_scalar, u, first, last):
-            lines, rows = slice(first // LINE, last // LINE), slice(2 * u, 2 * u + 2)
-            if on_scalar:
-                nc.scalar.copy(out=targets[:, lines, rows], in_=w_columns[:, lines, rows])
-            else:
-                nc.gpsimd.tensor_scalar(targets[:, lines, rows], w_columns[:, lines, rows], 1.0, 0.0, ALU.mult, ALU.add)
+        def interleave(u, tiles):
+            rows = slice(2 * u, 2 * u + 2)
+            nc.scalar.copy(out=targets[:, tiles, :split, rows], in_=w_columns[:, tiles, :split, rows])
+            nc.vector.tensor_copy(targets[:, tiles, split:, rows], w_columns[:, tiles, split:, rows])
 
         def quantize(c):
             nc.vector.quantize_mx(
@@ -102,16 +100,13 @@ def tile_picked_pick_lin_relu2_srt_p_kernel(tc, x_words, x_scales, w, b, offs, o
             )
 
         nc.vector.tensor_copy(scale_table[live(STAGED), :].bitcast(I32), first_rows[live(STAGED), :])
+        interleave(0, slice(0, M_TILES))
         nc.vector.tensor_copy(x_scale[:], scale_table[:].indirect(offsets[:]))
-
-        interleave(True, 0, 0, SCALAR_COLUMNS)
-        interleave(False, 0, SCALAR_COLUMNS, N)
-        interleave(True, 1, 0, P)
-        interleave(False, 1, SCALAR_COLUMNS, N)
-        interleave(True, 1, P, SCALAR_COLUMNS)
-        quantize(0)
+        for c in range(M_TILES):
+            interleave(1, slice(c, c + 1))
+        for c in range(M_TILES):
+            quantize(c)
         gather_words(early_codes[:], 0)
-        quantize(1)
         late_codes = keep.tile([P, S - CHUNK], U32, name="late_codes", tag="raw", align_bytes=64)
         for i in range(1, CHUNKS):
             gather_words(late_codes[:, tokens(i - 1)], i)

@@ -20,12 +20,12 @@ PACK = 4
 QUADRANT = 32
 LIST_ROWS = 16
 M_TILES = N // P
-LINE = 4
 STAGED = 2
 BLOCK = 8
 CHUNK = 128
 CHUNKS = S // CHUNK
-SCALAR_COLUMNS = 80
+SCALAR_LOW = 80
+SCALAR_HIGH = 48
 
 
 def reach(i):
@@ -85,14 +85,7 @@ def tile_picked_pick_lin_relu2_srt_p_kernel(tc, x_words, x_scales, w, b, offs, o
             entries = slice(i * CHUNK // LIST_ROWS, (i + 1) * CHUNK // LIST_ROWS)
             nc.vector.tensor_copy(codes, word_table[:, : reach(i)].bitcast(U32).indirect(offsets[:, entries]))
 
-        w_columns = w_raw[:].rearrange("p t (c j i) -> p c j t i", c=M_TILES, i=LINE)
-        targets = grouped[:].rearrange("p c (j i) t -> p c j t i", i=LINE)
-        split = SCALAR_COLUMNS // LINE
-
-        def interleave(u, tiles):
-            rows = slice(2 * u, 2 * u + 2)
-            nc.scalar.copy(out=targets[:, tiles, :split, rows], in_=w_columns[:, tiles, :split, rows])
-            nc.vector.tensor_copy(targets[:, tiles, split:, rows], w_columns[:, tiles, split:, rows])
+        w_columns = w_raw[:].rearrange("p t (c m) -> p c m t", c=M_TILES)
 
         def quantize(c):
             nc.vector.quantize_mx(
@@ -100,10 +93,15 @@ def tile_picked_pick_lin_relu2_srt_p_kernel(tc, x_words, x_scales, w, b, offs, o
             )
 
         nc.vector.tensor_copy(scale_table[live(STAGED), :].bitcast(I32), first_rows[live(STAGED), :])
-        interleave(0, slice(0, M_TILES))
+
+        def interleave(tiles, rows, split):
+            nc.scalar.copy(out=grouped[:, tiles, :split, rows], in_=w_columns[:, tiles, :split, rows])
+            nc.vector.tensor_copy(grouped[:, tiles, split:, rows], w_columns[:, tiles, split:, rows])
+
+        interleave(slice(0, M_TILES), slice(0, 2), SCALAR_LOW)
         nc.vector.tensor_copy(x_scale[:], scale_table[:].indirect(offsets[:]))
         for c in range(M_TILES):
-            interleave(1, slice(c, c + 1))
+            interleave(slice(c, c + 1), slice(2, PACK), SCALAR_HIGH)
         for c in range(M_TILES):
             quantize(c)
         gather_words(early_codes[:], 0)
@@ -127,15 +125,12 @@ def tile_picked_pick_lin_relu2_srt_p_kernel(tc, x_words, x_scales, w, b, offs, o
                 start=True,
                 stop=True,
             )
-            nc.scalar.activation(biased[:, c, tokens(i)], acc[:], ACT.Relu, bias=bias[:, c, 0:1])
+            nc.scalar.activation(biased[:, c, tokens(i)], acc[:], ACT.Identity, bias=bias[:, c, 0:1])
 
         stored = [0] * M_TILES
         for n, (i, c) in enumerate(order):
             v = biased[:, c, tokens(i)]
-            if n == len(order) - 2:
-                nc.scalar.activation(y[:, c, tokens(i)], v, ACT.Square, bias=zero[:])
-            else:
-                nc.vector.tensor_tensor(y[:, c, tokens(i)], v, v, ALU.mult)
+            nc.vector.scalar_tensor_tensor(y[:, c, tokens(i)], v, zero[:], v, ALU.max, ALU.mult)
             if n + 1 == len(order) or order[n + 1][1] != c:
                 run = tokens(stored[c], i)
                 nc.sync.dma_start(out=out_rows[:, c, run], in_=y[:, c, run])

@@ -25,7 +25,7 @@ BLOCK = 8
 CHUNK = 128
 CHUNKS = S // CHUNK
 SCALAR_LOW = 80
-SCALAR_HIGH = 48
+SCALAR_HIGH = (96, 64)
 
 
 def reach(i):
@@ -101,7 +101,7 @@ def tile_picked_pick_lin_relu2_srt_p_kernel(tc, x_words, x_scales, w, b, offs, o
         interleave(slice(0, M_TILES), slice(0, 2), SCALAR_LOW)
         nc.vector.tensor_copy(x_scale[:], scale_table[:].indirect(offsets[:]))
         for c in range(M_TILES):
-            interleave(slice(c, c + 1), slice(2, PACK), SCALAR_HIGH)
+            interleave(slice(c, c + 1), slice(2, PACK), SCALAR_HIGH[c])
         for c in range(M_TILES):
             quantize(c)
         gather_words(early_codes[:], 0)

@@ -20,12 +20,12 @@ PACK = 4
 QUADRANT = 32
 LIST_ROWS = 16
 M_TILES = N // P
-STAGED = 2
+STAGED = 0
 BLOCK = 8
 CHUNK = 128
 CHUNKS = S // CHUNK
-SCALAR_LOW = 80
-SCALAR_HIGH = (96, 64)
+SCALAR_LOW = 104
+SCALAR_HIGH = (88, 56)
 
 
 def reach(i):
@@ -64,7 +64,7 @@ def tile_picked_pick_lin_relu2_srt_p_kernel(tc, x_words, x_scales, w, b, offs, o
         nc.sync.dma_start(out=w_raw[:, :2], in_=w_rows[:, :2])
         nc.sync.dma_start(offsets[:], offs)
         nc.vector.memset(scale_table[:].bitcast(I32), 0)
-        for q in (0, 3, 1):
+        for q in (2, 1, 3):
             nc.sync.dma_start(out=scale_table[live(q), :].bitcast(I32), in_=scale_rows(q))
         nc.sync.dma_start(out=w_raw[:, 2:], in_=w_rows[:, 2:])
         for first, last in ((0, reach(0)), (reach(0), reach(2)), (reach(2), T)):

from contextlib import ExitStack

import concourse.mybir as mybir

K, T, S, N = 512, 1024, 512, 256
FLOPS = 2 * K * S * N

F32 = mybir.dt.float32
BF16 = mybir.dt.bfloat16
I32 = mybir.dt.int32
U32 = mybir.dt.uint32
U16 = mybir.dt.uint16
U8 = mybir.dt.uint8
FP8X4 = mybir.dt.float8_e4m3fn_x4
ACT = mybir.ActivationFunctionType
ALU = mybir.AluOpType

P = 128
PACK = 4
QUADRANT = 32
LIST_ROWS = 16
M_TILES = N // P
STAGED = 0
BLOCK = 8
CHUNK = 128
CHUNKS = S // CHUNK
SCALAR_LOW = 104
SCALAR_HIGH = (88, 56)


def reach(i):
    return T - S + (i + 1) * CHUNK


def tokens(first, last=None):
    return slice(first * CHUNK, ((first if last is None else last) + 1) * CHUNK)


def tile_picked_pick_lin_relu2_srt_p_kernel(tc, x_words, x_scales, w, b, offs, out):
    nc = tc.nc
    with ExitStack() as ctx:
        keep = ctx.enter_context(tc.tile_pool(name="keep", bufs=1))
        psum = ctx.enter_context(tc.psum_pool(name="psum", bufs=1))

        offsets = keep.tile([P, S // LIST_ROWS], U16, name="offsets")
        w_raw = keep.tile([P, PACK, N], F32, name="w_raw", tag="raw", align_bytes=64)
        word_table = keep.tile([P, T], I32, name="word_table", align_bytes=64)
        scale_table = keep.tile([P, T], U8, name="scale_table", align_bytes=64)
        first_rows = keep.tile([P, T // PACK], I32, name="first_rows", align_bytes=64)
        bias = keep.tile([P, M_TILES, BLOCK], F32, name="bias")
        zero_in = keep.tile([P, 1], F32, name="zero_in")
        zero = keep.tile([P, 1], F32, name="zero")

        words = x_words[0].rearrange("p c r -> p (c r)").bitcast(I32)
        w_rows = w.rearrange("(p t) n -> p t n", t=PACK)

        def live(q):
            return slice(QUADRANT * q, QUADRANT * q + 4)

        def scale_rows(q):
            return x_scales[0, 4 * q : 4 * q + 4, :].bitcast(I32)

        nc.scalar.dma_start(out=first_rows[live(STAGED), :], in_=scale_rows(STAGED))
        nc.sync.dma_start(out=w_raw[:, :2], in_=w_rows[:, :2])
        nc.sync.dma_start(offsets[:], offs)
        nc.vector.memset(scale_table[:].bitcast(I32), 0)
        for q in (2, 1, 3):
            nc.sync.dma_start(out=scale_table[live(q), :].bitcast(I32), in_=scale_rows(q))
        nc.sync.dma_start(out=w_raw[:, 2:], in_=w_rows[:, 2:])
        for first, last in ((0, reach(0)), (reach(0), reach(2)), (reach(2), T)):
            nc.sync.dma_start(out=word_table[:, first:last], in_=words[:, first:last])
        with nc.allow_non_contiguous_dma(reason="two bias values a partition"):
            nc.sync.dma_start(out=bias[:, :, 0:1], in_=b.rearrange("(c p) o -> p c o", c=M_TILES))

        nc.vector.memset(zero_in[:], 0.0)
        nc.scalar.activation(zero[:], zero_in[:], ACT.Identity)

        x_scale = keep.tile([P, S], U8, name="x_scale", align_bytes=64)
        early_codes = keep.tile([P, CHUNK], U32, name="early_codes", align_bytes=64)
        grouped = keep.tile([P, M_TILES, P, PACK], BF16, name="grouped", tag="stage", align_bytes=64)
        w_scale = [keep.tile([P, P], U8, name="w_scale%d" % c, align_bytes=64) for c in range(M_TILES)]
        w_codes = [keep.tile([P, P], U32, name="w_codes%d" % c, align_bytes=64) for c in range(M_TILES)]

        def gather_words(codes, i):
            entries = slice(i * CHUNK // LIST_ROWS, (i + 1) * CHUNK // LIST_ROWS)
            nc.vector.tensor_copy(codes, word_table[:, : reach(i)].bitcast(U32).indirect(offsets[:, entries]))

        w_columns = w_raw[:].rearrange("p t (c m) -> p c m t", c=M_TILES)

        def quantize(c):
            nc.vector.quantize_mx(
                out=w_codes[c][:].bitcast(FP8X4), scales=w_scale[c][:], in_=grouped[:, c].rearrange("p m t -> p (m t)")
            )

        nc.vector.tensor_copy(scale_table[live(STAGED), :].bitcast(I32), first_rows[live(STAGED), :])

        def interleave(tiles, rows, split):
            nc.scalar.copy(out=grouped[:, tiles, :split, rows], in_=w_columns[:, tiles, :split, rows])
            nc.vector.tensor_copy(grouped[:, tiles, split:, rows], w_columns[:, tiles, split:, rows])

        interleave(slice(0, M_TILES), slice(0, 2), SCALAR_LOW)
        nc.vector.tensor_copy(x_scale[:], scale_table[:].indirect(offsets[:]))
        for c in range(M_TILES):
            interleave(slice(c, c + 1), slice(2, PACK), SCALAR_HIGH[c])
        for c in range(M_TILES):
            quantize(c)
        gather_words(early_codes[:], 0)
        late_codes = keep.tile([P, S - CHUNK], U32, name="late_codes", tag="raw", align_bytes=64)
        for i in range(1, CHUNKS):
            gather_words(late_codes[:, tokens(i - 1)], i)

        out_rows = out.rearrange("(c p) s -> p c s", c=M_TILES)
        y = keep.tile([P, M_TILES, S], F32, name="y", tag="stage", align_bytes=64)
        biased = keep.tile([P, M_TILES, S], F32, name="biased")

        order = [(i, c if i % 2 == 0 else M_TILES - 1 - c) for i in range(CHUNKS) for c in range(M_TILES)]
        for i, c in order:
            acc = psum.tile([P, CHUNK], F32, name="acc%d_%d" % (i, c))
            nc.tensor.matmul_mx(
                out=acc[:],
                lhsT=w_codes[c][:].bitcast(FP8X4),
                lhsT_scale=w_scale[c][:],
                rhs=(late_codes[:, tokens(i - 1)] if i else early_codes[:]).bitcast(FP8X4),
                rhs_scale=x_scale[:, tokens(i)],
                start=True,
                stop=True,
            )
            nc.scalar.activation(biased[:, c, tokens(i)], acc[:], ACT.Identity, bias=bias[:, c, 0:1])

        stored = [0] * M_TILES
        for n, (i, c) in enumerate(order):
            v = biased[:, c, tokens(i)]
            nc.vector.scalar_tensor_tensor(y[:, c, tokens(i)], v, zero[:], v, ALU.max, ALU.mult)
            if n + 1 == len(order) or order[n + 1][1] != c:
                run = tokens(stored[c], i)
                nc.sync.dma_start(out=out_rows[:, c, run], in_=y[:, c, run])
                stored[c] = i + 1
